import numpy as np
import ml_dtypes


def mxq(x, axis, fmt="e4m3"):
    dtype, down = {"e4m3": (ml_dtypes.float8_e4m3fn, 7), "e5m2": (ml_dtypes.float8_e5m2, 14)}[fmt]
    v = np.moveaxis(np.asarray(x, np.float32).astype(ml_dtypes.bfloat16).astype(np.float64), axis, -1)
    blocks = v.reshape(v.shape[:-1] + (-1, 32))
    amax = np.abs(blocks).max(-1, keepdims=True)
    byte = np.maximum(np.where(amax > 0, np.frexp(amax)[1] - 1 + 127, 0) - down, 1)
    scale = np.exp2(byte - 127.0)
    codes = (blocks / scale).astype(np.float32).astype(dtype).astype(np.float64)
    return np.moveaxis((codes * scale).reshape(v.shape), -1, axis)


WIDE = False


def mx_kscale(k):
    if not WIDE:
        return np.ones(k)
    levels = np.array([10, -10, 5, -5, 0])
    if k % 512:
        return np.exp2(np.random.permutation(np.resize(levels, k // 32))).repeat(32)
    a = np.empty((k // 512, 16))
    for p in range(k // 512):
        a[p, :8] = np.random.permutation(np.resize(levels, 8))
        for g in range(8):
            far = levels[np.abs(levels - a[p, g]) >= 10]
            a[p, g + 8] = far[np.random.randint(len(far))]
    return np.exp2(a.ravel()).repeat(32)


def f64(x):
    return np.asarray(x).astype(np.float64)


def striped(idx):
    return np.tile(idx.reshape(-1, 16).T, (8, 1)).astype(np.uint16)


def unstriped(offs):
    return offs[:16].T.reshape(-1).astype(np.int64)


K, T, E, C, N = 1024, 512, 8, 128, 128


def by_expert(wq, xq):
    return np.concatenate([wq[e].T @ xq[:, e * C:(e + 1) * C] for e in range(E)], axis=1)


def setup_inputs():
    n = np.random.standard_normal
    s = mx_kscale(K)[:, None]
    first = np.random.permutation(np.repeat(np.arange(E), T // E))
    second = (first + 1 + np.random.permutation(np.repeat(np.arange(E - 1), -(-T // (E - 1)))[:T])) % E
    while np.bincount(second, minlength=E).max() != T // E:
        load = np.bincount(second, minlength=E); hi, lo = int(load.argmax()), int(load.argmin())
        t = np.flatnonzero((second == hi) & (first != lo))[0]; second[t] = lo
    slot_token = np.empty(E * C, np.int64); pos = np.empty((2, T), np.int64); fill = np.zeros(E, np.int64)
    place = np.stack([np.random.permutation(C) for _ in range(E)])
    for r, deal in enumerate((first, second)):
        for t in np.random.permutation(T):
            e = deal[t]; j = e * C + place[e, fill[e]]; fill[e] += 1; slot_token[j] = t; pos[r, t] = j
    g = np.random.uniform(0.2, 0.8, T)
    return {
        "xT": (n((K, T)) * s).astype(np.float32),
        "w": (n((E, K, N)) / np.sqrt(K) / s[None]).astype(np.float32),
        "b": (0.3 * n((N, E))).astype(np.float32),
        "gate": np.stack([np.tile(g, (N, 1)), np.tile(1.0 - g, (N, 1))]).astype(np.float32),
        "offs": striped(slot_token),
        "pos1": striped(pos[0]),
        "pos2": striped(pos[1]),
    }


def reference(xT, w, b, gate, offs, pos1, pos2):
    idx = unstriped(offs)
    xq = mxq(f64(xT)[:, idx], 0, "e4m3")
    y = by_expert(mxq(f64(w), 1, "e4m3"), xq)
    y = y + np.repeat(f64(b), C, axis=1)
    return f64(gate[0]) * y[:, unstriped(pos1)] + f64(gate[1]) * y[:, unstriped(pos2)]

@@ -1,0 +1,149 @@
+from contextlib import ExitStack
+
+import concourse.mybir as mybir
+
+K, T, E, C, N = 1024, 512, 8, 128, 128
+FLOPS = 2 * K * E * C * N
+
+F32 = mybir.dt.float32
+BF16 = mybir.dt.bfloat16
+U32 = mybir.dt.uint32
+I32 = mybir.dt.int32
+U16 = mybir.dt.uint16
+U8 = mybir.dt.uint8
+FP8X4 = mybir.dt.float8_e4m3fn_x4
+MULT = mybir.AluOpType.mult
+IDENTITY = mybir.ActivationFunctionType.Identity
+
+P = 128
+PACK = 4
+PASSES = K // (P * PACK)
+HALF = T // 2
+WINDOW = 1376
+X_SPLIT = (64, 112, 256, 256)
+LOADS = tuple((2 * e, 2) for e in range(E - 1)) + ((14, 1), (15, 1))
+GROUPS = ((0, 2), (2, 2), (4, 2), (6, 1), (7, 1))
+VECTOR_EXPERTS = (4, 6)
+CUT = 320
+
+
+def tile_routed_moe_kernel(tc, xT, w, b, gate, offs, pos1, pos2, out):
+    nc = tc.nc
+    x_view = xT.rearrange("(a p j) t -> a p j t", p=P, j=PACK)
+    w_view = w.rearrange("e (a p j) n -> p (e a) (j n)", p=P, j=PACK)
+
+    def interleave(copy, dst, src):
+        if len(src.shape) == 3:
+            copy(out=dst.rearrange("p (c i) t -> p c t i", i=4), in_=src.rearrange("p t (c i) -> p c t i", i=4))
+        else:
+            copy(out=dst.rearrange("p a (c i) t -> p a c t i", i=4), in_=src.rearrange("p a t (c i) -> p a c t i", i=4))
+
+    with ExitStack() as ctx:
+        keep = ctx.enter_context(tc.tile_pool(name="keep", bufs=1))
+        psum = ctx.enter_context(tc.psum_pool(name="psum", bufs=1))
+
+        offs_t = keep.tile([P, E * C // 16], U16, name="offs_t")
+        pos1_t = keep.tile([P, T // 16], U16, name="pos1_t")
+        pos2_t = keep.tile([P, T // 16], U16, name="pos2_t")
+        bias = keep.tile([P, E], F32, name="bias")
+        gates = keep.tile([P, 2, T], F32, name="gates")
+
+        x_scales = keep.tile([P, WINDOW], U8, name="x_scales", align_bytes=64)
+        nc.gpsimd.memset(x_scales[:], 0)
+        x_words = []
+        for a in range(PASSES):
+            words = keep.tile([P, WINDOW], I32, name=f"x_words{a}", align_bytes=64)
+            nc.vector.memset(words[:, T:WINDOW], 0)
+            x_words.append(words)
+
+        x_raw = {}
+        for a, h, width in ((0, 0, 1), (0, 1, 1), (1, 0, 1), (1, 1, 1)):
+            raw = keep.tile([P, PACK, width * HALF], F32, name=f"x_raw{a}{h}")
+            nc.sync.dma_start(out=raw[:], in_=x_view[a, :, :, h * HALF : (h + width) * HALF])
+            x_raw[a, h] = raw
+            if (a, h) == (0, 1):
+                nc.sync.dma_start(offs_t[:], offs)
+        w_raw = []
+        for first, count in LOADS:
+            raw = keep.tile([P, count, PACK, N], F32, name=f"w_raw{first}")
+            nc.sync.dma_start(out=raw[:].rearrange("p s j n -> p s (j n)"), in_=w_view[:, first : first + count])
+            for i in range(0, count, PASSES):
+                w_raw.append(raw[:, i : i + PASSES] if count > 1 else raw)
+        nc.sync.dma_start(bias[:], b)
+        nc.sync.dma_start(pos1_t[:], pos1)
+        nc.sync.dma_start(pos2_t[:], pos2)
+        nc.sync.dma_start(out=gates[:], in_=gate.rearrange("g p t -> p g t"))
+
+        g_words = []
+        for a in range(PASSES):
+            for h in range(2):
+                cols = slice(h * HALF, (h + 1) * HALF)
+                grouped = keep.tile([P, HALF, PACK], BF16, name=f"x_grouped{a}{h}", align_bytes=64)
+                split = X_SPLIT[2 * a + h]
+                if split > 0:
+                    interleave(nc.scalar.copy, grouped[:, 0:split], x_raw[a, h][:, :, 0:split])
+                if split < HALF:
+                    interleave(nc.vector.tensor_copy, grouped[:, split:HALF], x_raw[a, h][:, :, split:HALF])
+                nc.vector.quantize_mx(
+                    out=x_words[a][:, cols].bitcast(FP8X4),
+                    scales=x_scales[4 * a : P, cols],
+                    in_=grouped[:].rearrange("p w t -> p (w t)"),
+                )
+            gathered = keep.tile([P, E * C], U32, name=f"g_words{a}", align_bytes=64)
+            nc.vector.tensor_copy(out=gathered[:], in_=x_words[a][:].bitcast(U32).indirect(offs_t[:]))
+            g_words.append(gathered)
+        g_scales = keep.tile([P, E * C], U8, name="g_scales", align_bytes=64)
+        for lo, hi in ((0, 512), (512, 1024)):
+            nc.vector.tensor_copy(out=g_scales[:, lo:hi], in_=x_scales[:].indirect(offs_t[:, lo // 16 : hi // 16]))
+
+        y = keep.tile([P, E * C], F32, name="y")
+        for first, count in GROUPS:
+            grouped = keep.tile([P, count, PASSES, N, PACK], BF16, name=f"w_grouped{first}", align_bytes=64)
+            words = keep.tile([P, count, PASSES, N], U32, name=f"w_words{first}", align_bytes=64)
+            scales = keep.tile([P, count, PASSES, N], U8, name=f"w_scales{first}", align_bytes=64)
+            for i in range(count):
+                e = first + i
+                if e == E - 1:
+                    interleave(nc.scalar.copy, grouped[:, i, 0], w_raw[e][:, 0])
+                    interleave(nc.vector.tensor_copy, grouped[:, i, 1], w_raw[e + 1][:, 0])
+                elif e in VECTOR_EXPERTS:
+                    interleave(nc.vector.tensor_copy, grouped[:, i], w_raw[e][:])
+                else:
+                    interleave(nc.scalar.copy, grouped[:, i], w_raw[e][:])
+            pieces = PASSES if first == E - 1 else 1
+            width = count * PASSES * N // pieces
+            for q in range(pieces):
+                cols = slice(q * width, (q + 1) * width)
+                nc.vector.quantize_mx(
+                    out=words[:].rearrange("p e a n -> p (e a n)")[:, cols].bitcast(FP8X4),
+                    scales=scales[:].rearrange("p e a n -> p (e a n)")[:, cols],
+                    in_=grouped[:].rearrange("p e a n t -> p (e a n t)")[:, q * width * PACK : (q + 1) * width * PACK],
+                )
+            for i in range(count):
+                e = first + i
+                slots = slice(e * C, (e + 1) * C)
+                acc = psum.tile([P, C], F32, name=f"acc{e}")
+                for a in range(PASSES):
+                    nc.tensor.matmul_mx(
+                        out=acc[:],
+                        lhsT=words[:, i, a, :].bitcast(FP8X4),
+                        lhsT_scale=scales[:, i, a, :],
+                        rhs=g_words[a][:, slots].bitcast(FP8X4),
+                        rhs_scale=g_scales[4 * a : P, slots],
+                        start=(a == 0),
+                        stop=(a == PASSES - 1),
+                    )
+                nc.scalar.activation(y[:, slots], acc[:], IDENTITY, bias=bias[:, e : e + 1])
+
+        part1 = keep.tile([P, T], F32, name="part1")
+        nc.vector.tensor_tensor(part1[:], y[:].indirect(pos1_t[:]), gates[:, 0, :], MULT)
+        pieces = ((0, CUT), (CUT, T))
+        part2 = []
+        for lo, hi in pieces:
+            part = keep.tile([P, hi - lo], F32, name=f"part2_{lo}")
+            nc.vector.tensor_tensor(part[:], y[:].indirect(pos2_t[:, lo // 16 : hi // 16]), gates[:, 1, lo:hi], MULT)
+            part2.append(part)
+        for (lo, hi), part in zip(pieces, part2):
+            total = keep.tile([P, hi - lo], F32, name=f"total{lo}")
+            nc.vector.tensor_add(total[:], part1[:, lo:hi], part[:])
+            nc.sync.dma_start(out=out[:, lo:hi], in_=total[:])

@@ -13,6 +13,7 @@ U16 = mybir.dt.uint16
 U8 = mybir.dt.uint8
 FP8X4 = mybir.dt.float8_e4m3fn_x4
 MULT = mybir.AluOpType.mult
+ADD = mybir.AluOpType.add
 IDENTITY = mybir.ActivationFunctionType.Identity
 
 P = 128
@@ -20,17 +21,15 @@ PACK = 4
 PASSES = K // (P * PACK)
 HALF = T // 2
 WINDOW = 1376
-X_SPLIT = (64, 112, 256, 256)
-LOADS = tuple((2 * e, 2) for e in range(E - 1)) + ((14, 1), (15, 1))
-GROUPS = ((0, 2), (2, 2), (4, 2), (6, 1), (7, 1))
-VECTOR_EXPERTS = (4, 6)
+X0_SCALAR = 176
+X1_VECTOR = 128
 CUT = 320
 
 
 def tile_routed_moe_kernel(tc, xT, w, b, gate, offs, pos1, pos2, out):
     nc = tc.nc
     x_view = xT.rearrange("(a p j) t -> a p j t", p=P, j=PACK)
-    w_view = w.rearrange("e (a p j) n -> p (e a) (j n)", p=P, j=PACK)
+    w_view = w.rearrange("e (a p j) n -> p e a (j n)", p=P, j=PACK)
 
     def interleave(copy, dst, src):
         if len(src.shape) == 3:
@@ -46,7 +45,8 @@ def tile_routed_moe_kernel(tc, xT, w, b, gate, offs, pos1, pos2, out):
         pos1_t = keep.tile([P, T // 16], U16, name="pos1_t")
         pos2_t = keep.tile([P, T // 16], U16, name="pos2_t")
         bias = keep.tile([P, E], F32, name="bias")
-        gates = keep.tile([P, 2, T], F32, name="gates")
+        gate1 = keep.tile([P, T], F32, name="gate1")
+        gate2 = keep.tile([P, T], F32, name="gate2")
 
         x_scales = keep.tile([P, WINDOW], U8, name="x_scales", align_bytes=64)
         nc.gpsimd.memset(x_scales[:], 0)
@@ -56,92 +56,113 @@ def tile_routed_moe_kernel(tc, xT, w, b, gate, offs, pos1, pos2, out):
             nc.vector.memset(words[:, T:WINDOW], 0)
             x_words.append(words)
 
-        x_raw = {}
-        for a, h, width in ((0, 0, 1), (0, 1, 1), (1, 0, 1), (1, 1, 1)):
-            raw = keep.tile([P, PACK, width * HALF], F32, name=f"x_raw{a}{h}")
-            nc.sync.dma_start(out=raw[:], in_=x_view[a, :, :, h * HALF : (h + width) * HALF])
-            x_raw[a, h] = raw
-            if (a, h) == (0, 1):
-                nc.sync.dma_start(offs_t[:], offs)
+        x0_raw = keep.tile([P, PACK, T], F32, name="x0_raw")
+        nc.sync.dma_start(out=x0_raw[:], in_=x_view[0])
+        nc.sync.dma_start(offs_t[:], offs)
+        x1_raw = keep.tile([P, PACK, T], F32, name="x1_raw")
+        nc.sync.dma_start(out=x1_raw[:], in_=x_view[1])
         w_raw = []
-        for first, count in LOADS:
-            raw = keep.tile([P, count, PACK, N], F32, name=f"w_raw{first}")
-            nc.sync.dma_start(out=raw[:].rearrange("p s j n -> p s (j n)"), in_=w_view[:, first : first + count])
-            for i in range(0, count, PASSES):
-                w_raw.append(raw[:, i : i + PASSES] if count > 1 else raw)
-        nc.sync.dma_start(bias[:], b)
-        nc.sync.dma_start(pos1_t[:], pos1)
-        nc.sync.dma_start(pos2_t[:], pos2)
-        nc.sync.dma_start(out=gates[:], in_=gate.rearrange("g p t -> p g t"))
-
-        g_words = []
+        for e in range(E - 1):
+            raw = keep.tile([P, PASSES, PACK, N], F32, name=f"w_raw{e}", tag=f"w_raw{e}")
+            nc.sync.dma_start(out=raw[:].rearrange("p a j n -> p a (j n)"), in_=w_view[:, e])
+            w_raw.append(raw)
+            if e == 2:
+                nc.sync.dma_start(bias[:], b)
+        last_raw = []
         for a in range(PASSES):
-            for h in range(2):
-                cols = slice(h * HALF, (h + 1) * HALF)
-                grouped = keep.tile([P, HALF, PACK], BF16, name=f"x_grouped{a}{h}", align_bytes=64)
-                split = X_SPLIT[2 * a + h]
-                if split > 0:
-                    interleave(nc.scalar.copy, grouped[:, 0:split], x_raw[a, h][:, :, 0:split])
-                if split < HALF:
-                    interleave(nc.vector.tensor_copy, grouped[:, split:HALF], x_raw[a, h][:, :, split:HALF])
-                nc.vector.quantize_mx(
-                    out=x_words[a][:, cols].bitcast(FP8X4),
-                    scales=x_scales[4 * a : P, cols],
-                    in_=grouped[:].rearrange("p w t -> p (w t)"),
-                )
+            raw = keep.tile([P, PACK, N], F32, name=f"last_raw{a}")
+            nc.sync.dma_start(out=raw[:].rearrange("p j n -> p (j n)"), in_=w_view[:, E - 1, a])
+            last_raw.append(raw)
+        nc.sync.dma_start(pos1_t[:], pos1)
+        nc.sync.dma_start(gate1[:], gate[0])
+        nc.sync.dma_start(pos2_t[:], pos2)
+        nc.sync.dma_start(gate2[:], gate[1])
+
+        def quantize_tokens(a, h, grouped):
+            cols = slice(h * HALF, (h + 1) * HALF)
+            nc.vector.quantize_mx(
+                out=x_words[a][:, cols].bitcast(FP8X4),
+                scales=x_scales[4 * a : P, cols],
+                in_=grouped[:].rearrange("p w t -> p (w t)"),
+            )
+
+        def gather_words(a):
             gathered = keep.tile([P, E * C], U32, name=f"g_words{a}", align_bytes=64)
             nc.vector.tensor_copy(out=gathered[:], in_=x_words[a][:].bitcast(U32).indirect(offs_t[:]))
-            g_words.append(gathered)
+            return gathered
+
+        g_words = []
+        x0_grouped = [keep.tile([P, HALF, PACK], BF16, name=f"x0_grouped{h}", align_bytes=64) for h in range(2)]
+        interleave(nc.scalar.copy, x0_grouped[0][:, 0:X0_SCALAR], x0_raw[:, :, 0:X0_SCALAR])
+        interleave(nc.vector.tensor_copy, x0_grouped[1][:], x0_raw[:, :, HALF:T])
+        interleave(nc.vector.tensor_copy, x0_grouped[0][:, X0_SCALAR:HALF], x0_raw[:, :, X0_SCALAR:HALF])
+        for h in (1, 0):
+            quantize_tokens(0, h, x0_grouped[h])
+        g_words.append(gather_words(0))
+        x1_grouped = [keep.tile([P, HALF, PACK], BF16, name=f"x1_grouped{h}", align_bytes=64) for h in range(2)]
+        split = HALF - X1_VECTOR
+        interleave(nc.scalar.copy, x1_grouped[0][:], x1_raw[:, :, 0:HALF])
+        interleave(nc.scalar.copy, x1_grouped[1][:, 0:split], x1_raw[:, :, HALF : HALF + split])
+        interleave(nc.vector.tensor_copy, x1_grouped[1][:, split:HALF], x1_raw[:, :, HALF + split : T])
+        for h in range(2):
+            quantize_tokens(1, h, x1_grouped[h])
+        g_words.append(gather_words(1))
         g_scales = keep.tile([P, E * C], U8, name="g_scales", align_bytes=64)
         for lo, hi in ((0, 512), (512, 1024)):
             nc.vector.tensor_copy(out=g_scales[:, lo:hi], in_=x_scales[:].indirect(offs_t[:, lo // 16 : hi // 16]))
 
-        y = keep.tile([P, E * C], F32, name="y")
-        for first, count in GROUPS:
-            grouped = keep.tile([P, count, PASSES, N, PACK], BF16, name=f"w_grouped{first}", align_bytes=64)
-            words = keep.tile([P, count, PASSES, N], U32, name=f"w_words{first}", align_bytes=64)
-            scales = keep.tile([P, count, PASSES, N], U8, name=f"w_scales{first}", align_bytes=64)
-            for i in range(count):
-                e = first + i
-                if e == E - 1:
-                    interleave(nc.scalar.copy, grouped[:, i, 0], w_raw[e][:, 0])
-                    interleave(nc.vector.tensor_copy, grouped[:, i, 1], w_raw[e + 1][:, 0])
-                elif e in VECTOR_EXPERTS:
-                    interleave(nc.vector.tensor_copy, grouped[:, i], w_raw[e][:])
-                else:
-                    interleave(nc.scalar.copy, grouped[:, i], w_raw[e][:])
-            pieces = PASSES if first == E - 1 else 1
-            width = count * PASSES * N // pieces
-            for q in range(pieces):
-                cols = slice(q * width, (q + 1) * width)
-                nc.vector.quantize_mx(
-                    out=words[:].rearrange("p e a n -> p (e a n)")[:, cols].bitcast(FP8X4),
-                    scales=scales[:].rearrange("p e a n -> p (e a n)")[:, cols],
-                    in_=grouped[:].rearrange("p e a n t -> p (e a n t)")[:, q * width * PACK : (q + 1) * width * PACK],
+        w_grouped = keep.tile([P, E, PASSES, N, PACK], BF16, name="w_grouped", align_bytes=64)
+        w_words = keep.tile([P, E, PASSES, N], U32, name="w_words", align_bytes=64)
+        w_scales = keep.tile([P, E, PASSES, N], U8, name="w_scales", align_bytes=64)
+        acc = [psum.tile([P, C], F32, name=f"acc{e}") for e in range(E)]
+
+        def quantize_weights(first, count):
+            cols = slice(first * N, (first + count) * N)
+            nc.vector.quantize_mx(
+                out=w_words[:].rearrange("p e a n -> p (e a n)")[:, cols].bitcast(FP8X4),
+                scales=w_scales[:].rearrange("p e a n -> p (e a n)")[:, cols],
+                in_=w_grouped[:].rearrange("p e a n t -> p (e a n t)")[:, first * N * PACK : (first + count) * N * PACK],
+            )
+
+        def multiply(e):
+            slots = slice(e * C, (e + 1) * C)
+            for a in range(PASSES):
+                nc.tensor.matmul_mx(
+                    out=acc[e][:],
+                    lhsT=w_words[:, e, a, :].bitcast(FP8X4),
+                    lhsT_scale=w_scales[:, e, a, :],
+                    rhs=g_words[a][:, slots].bitcast(FP8X4),
+                    rhs_scale=g_scales[4 * a : P, slots],
+                    start=(a == 0),
+                    stop=(a == PASSES - 1),
                 )
-            for i in range(count):
-                e = first + i
-                slots = slice(e * C, (e + 1) * C)
-                acc = psum.tile([P, C], F32, name=f"acc{e}")
-                for a in range(PASSES):
-                    nc.tensor.matmul_mx(
-                        out=acc[:],
-                        lhsT=words[:, i, a, :].bitcast(FP8X4),
-                        lhsT_scale=scales[:, i, a, :],
-                        rhs=g_words[a][:, slots].bitcast(FP8X4),
-                        rhs_scale=g_scales[4 * a : P, slots],
-                        start=(a == 0),
-                        stop=(a == PASSES - 1),
-                    )
-                nc.scalar.activation(y[:, slots], acc[:], IDENTITY, bias=bias[:, e : e + 1])
+
+        def add_bias(y, e):
+            nc.scalar.activation(y[:, e * C : (e + 1) * C], acc[e][:], IDENTITY, bias=bias[:, e : e + 1])
+
+        for e in range(6):
+            interleave(nc.scalar.copy, w_grouped[:, e], w_raw[e][:])
+        y = keep.tile([P, E * C], F32, name="y", tag="w_raw5")
+        for first in (0, 4, 8):
+            quantize_weights(first, 4)
+        interleave(nc.scalar.copy, w_grouped[:, 6, 0], w_raw[6][:, 0])
+        interleave(nc.vector.tensor_copy, w_grouped[:, 6, 1], w_raw[6][:, 1])
+        interleave(nc.scalar.copy, w_grouped[:, 7, 0], last_raw[0][:])
+        interleave(nc.vector.tensor_copy, w_grouped[:, 7, 1], last_raw[1][:])
+        quantize_weights(12, 2)
+        quantize_weights(14, 1)
+        quantize_weights(15, 1)
+        for e in range(E):
+            multiply(e)
+            add_bias(y, e)
 
         part1 = keep.tile([P, T], F32, name="part1")
-        nc.vector.tensor_tensor(part1[:], y[:].indirect(pos1_t[:]), gates[:, 0, :], MULT)
+        nc.vector.tensor_tensor(part1[:], y[:].indirect(pos1_t[:]), gate1[:], MULT)
         pieces = ((0, CUT), (CUT, T))
         part2 = []
         for lo, hi in pieces:
             part = keep.tile([P, hi - lo], F32, name=f"part2_{lo}")
-            nc.vector.tensor_tensor(part[:], y[:].indirect(pos2_t[:, lo // 16 : hi // 16]), gates[:, 1, lo:hi], MULT)
+            nc.vector.tensor_tensor(part[:], y[:].indirect(pos2_t[:, lo // 16 : hi // 16]), gate2[:, lo:hi], MULT)
             part2.append(part)
         for (lo, hi), part in zip(pieces, part2):
             total = keep.tile([P, hi - lo], F32, name=f"total{lo}")

@@ -22,8 +22,10 @@ PASSES = K // (P * PACK)
 HALF = T // 2
 WINDOW = 1376
 X0_SCALAR = 176
-X1_VECTOR = 128
+X1_VECTOR = 64
 CUT = 320
+WHOLE = 4
+GPSIMD_EXPERT = 2
 
 
 def tile_routed_moe_kernel(tc, xT, w, b, gate, offs, pos1, pos2, out):
@@ -62,17 +64,19 @@ def tile_routed_moe_kernel(tc, xT, w, b, gate, offs, pos1, pos2, out):
         x1_raw = keep.tile([P, PACK, T], F32, name="x1_raw")
         nc.sync.dma_start(out=x1_raw[:], in_=x_view[1])
         w_raw = []
-        for e in range(E - 1):
-            raw = keep.tile([P, PASSES, PACK, N], F32, name=f"w_raw{e}", tag=f"w_raw{e}")
-            nc.sync.dma_start(out=raw[:].rearrange("p a j n -> p a (j n)"), in_=w_view[:, e])
-            w_raw.append(raw)
-            if e == 2:
-                nc.sync.dma_start(bias[:], b)
-        last_raw = []
-        for a in range(PASSES):
-            raw = keep.tile([P, PACK, N], F32, name=f"last_raw{a}")
-            nc.sync.dma_start(out=raw[:].rearrange("p j n -> p (j n)"), in_=w_view[:, E - 1, a])
-            last_raw.append(raw)
+        for e in range(E):
+            if e < WHOLE:
+                raw = keep.tile([P, PASSES, PACK, N], F32, name=f"w_raw{e}", tag=f"w_raw{e}", align_bytes=64)
+                nc.sync.dma_start(out=raw[:].rearrange("p a j n -> p a (j n)"), in_=w_view[:, e])
+                w_raw.append(raw)
+            else:
+                halves = []
+                for a in range(PASSES):
+                    raw = keep.tile([P, PACK, N], F32, name=f"w_raw{e}{a}", tag=f"w_raw{e}{a}")
+                    nc.sync.dma_start(out=raw[:].rearrange("p j n -> p (j n)"), in_=w_view[:, e, a])
+                    halves.append(raw)
+                w_raw.append(halves)
+        nc.sync.dma_start(bias[:], b)
         nc.sync.dma_start(pos1_t[:], pos1)
         nc.sync.dma_start(gate1[:], gate[0])
         nc.sync.dma_start(pos2_t[:], pos2)
@@ -107,9 +111,14 @@ def tile_routed_moe_kernel(tc, xT, w, b, gate, offs, pos1, pos2, out):
         for h in range(2):
             quantize_tokens(1, h, x1_grouped[h])
         g_words.append(gather_words(1))
-        g_scales = keep.tile([P, E * C], U8, name="g_scales", align_bytes=64)
-        for lo, hi in ((0, 512), (512, 1024)):
-            nc.vector.tensor_copy(out=g_scales[:, lo:hi], in_=x_scales[:].indirect(offs_t[:, lo // 16 : hi // 16]))
+
+        def gather_scales(half, tag):
+            gathered = keep.tile([P, E * C // 2], U8, name=f"g_scales{half}", tag=tag, align_bytes=64)
+            cols = slice(half * E * C // 32, (half + 1) * E * C // 32)
+            nc.vector.tensor_copy(out=gathered[:], in_=x_scales[:].indirect(offs_t[:, cols]))
+            return gathered
+
+        g_scales = [gather_scales(0, "g_scales0")]
 
         w_grouped = keep.tile([P, E, PASSES, N, PACK], BF16, name="w_grouped", align_bytes=64)
         w_words = keep.tile([P, E, PASSES, N], U32, name="w_words", align_bytes=64)
@@ -126,30 +135,41 @@ def tile_routed_moe_kernel(tc, xT, w, b, gate, offs, pos1, pos2, out):
 
         def multiply(e):
             slots = slice(e * C, (e + 1) * C)
+            own = slice((e % 4) * C, (e % 4 + 1) * C)
             for a in range(PASSES):
                 nc.tensor.matmul_mx(
                     out=acc[e][:],
                     lhsT=w_words[:, e, a, :].bitcast(FP8X4),
                     lhsT_scale=w_scales[:, e, a, :],
                     rhs=g_words[a][:, slots].bitcast(FP8X4),
-                    rhs_scale=g_scales[4 * a : P, slots],
+                    rhs_scale=g_scales[e // 4][4 * a : P, own],
                     start=(a == 0),
                     stop=(a == PASSES - 1),
                 )
 
         def add_bias(y, e):
-            nc.scalar.activation(y[:, e * C : (e + 1) * C], acc[e][:], IDENTITY, bias=bias[:, e : e + 1])
+            slots = slice(e * C, (e + 1) * C)
+            nc.scalar.activation(y[:, slots], acc[e][:], IDENTITY, bias=bias[:, e : e + 1])
 
-        for e in range(6):
-            interleave(nc.scalar.copy, w_grouped[:, e], w_raw[e][:])
-        y = keep.tile([P, E * C], F32, name="y", tag="w_raw5")
-        for first in (0, 4, 8):
-            quantize_weights(first, 4)
-        interleave(nc.scalar.copy, w_grouped[:, 6, 0], w_raw[6][:, 0])
-        interleave(nc.vector.tensor_copy, w_grouped[:, 6, 1], w_raw[6][:, 1])
-        interleave(nc.scalar.copy, w_grouped[:, 7, 0], last_raw[0][:])
-        interleave(nc.vector.tensor_copy, w_grouped[:, 7, 1], last_raw[1][:])
+        for e in range(WHOLE):
+            if e == GPSIMD_EXPERT:
+                for a in range(PASSES):
+                    nc.gpsimd.tensor_scalar(
+                        w_grouped[:, e, a], w_raw[e][:, a].rearrange("p t n -> p n t"), 1.0, 0.0, MULT, ADD
+                    )
+            else:
+                interleave(nc.scalar.copy, w_grouped[:, e], w_raw[e][:])
+        for e in range(WHOLE, E):
+            for a in range(PASSES):
+                if (e, a) != (E - 1, PASSES - 1):
+                    interleave(nc.scalar.copy, w_grouped[:, e, a], w_raw[e][a][:])
+        y = keep.tile([P, E * C], F32, name="y", tag=f"w_raw{E - 1}0")
+        quantize_weights(0, 4)
+        g_scales.append(gather_scales(1, "w_raw1"))
+        quantize_weights(4, 4)
+        quantize_weights(8, 4)
         quantize_weights(12, 2)
+        interleave(nc.vector.tensor_copy, w_grouped[:, E - 1, 1], w_raw[E - 1][1][:])
         quantize_weights(14, 1)
         quantize_weights(15, 1)
         for e in range(E):

@@ -19,13 +19,15 @@ IDENTITY = mybir.ActivationFunctionType.Identity
 P = 128
 PACK = 4
 PASSES = K // (P * PACK)
+SLOTS = E * C
+LIST_ROWS = 16
+PLANE_STEP = 4
 HALF = T // 2
 WINDOW = 1376
-X0_SCALAR = 176
-X1_VECTOR = 64
-CUT = 320
-WHOLE = 4
-GPSIMD_EXPERT = 2
+PASS0_SCALAR = 176
+PASS1_VECTOR = 64
+WHOLE = 2
+FIRST_SHARED = 2
 
 
 def tile_routed_moe_kernel(tc, xT, w, b, gate, offs, pos1, pos2, out):
@@ -35,17 +37,17 @@ def tile_routed_moe_kernel(tc, xT, w, b, gate, offs, pos1, pos2, out):
 
     def interleave(copy, dst, src):
         if len(src.shape) == 3:
-            copy(out=dst.rearrange("p (c i) t -> p c t i", i=4), in_=src.rearrange("p t (c i) -> p c t i", i=4))
+            copy(out=dst.rearrange("p (c i) j -> p c j i", i=4), in_=src.rearrange("p j (c i) -> p c j i", i=4))
         else:
-            copy(out=dst.rearrange("p a (c i) t -> p a c t i", i=4), in_=src.rearrange("p a t (c i) -> p a c t i", i=4))
+            copy(out=dst.rearrange("p a (c i) j -> p a c j i", i=4), in_=src.rearrange("p a j (c i) -> p a c j i", i=4))
 
     with ExitStack() as ctx:
         keep = ctx.enter_context(tc.tile_pool(name="keep", bufs=1))
         psum = ctx.enter_context(tc.psum_pool(name="psum", bufs=1))
 
-        offs_t = keep.tile([P, E * C // 16], U16, name="offs_t")
-        pos1_t = keep.tile([P, T // 16], U16, name="pos1_t")
-        pos2_t = keep.tile([P, T // 16], U16, name="pos2_t")
+        offs_t = keep.tile([P, SLOTS // LIST_ROWS], U16, name="offs_t")
+        pos1_t = keep.tile([P, T // LIST_ROWS], U16, name="pos1_t")
+        pos2_t = keep.tile([P, T // LIST_ROWS], U16, name="pos2_t")
         bias = keep.tile([P, E], F32, name="bias")
         gate1 = keep.tile([P, T], F32, name="gate1")
         gate2 = keep.tile([P, T], F32, name="gate2")
@@ -63,128 +65,125 @@ def tile_routed_moe_kernel(tc, xT, w, b, gate, offs, pos1, pos2, out):
         nc.sync.dma_start(offs_t[:], offs)
         x1_raw = keep.tile([P, PACK, T], F32, name="x1_raw")
         nc.sync.dma_start(out=x1_raw[:], in_=x_view[1])
-        w_raw = []
-        for e in range(E):
-            if e < WHOLE:
-                raw = keep.tile([P, PASSES, PACK, N], F32, name=f"w_raw{e}", tag=f"w_raw{e}", align_bytes=64)
-                nc.sync.dma_start(out=raw[:].rearrange("p a j n -> p a (j n)"), in_=w_view[:, e])
-                w_raw.append(raw)
-            else:
-                halves = []
-                for a in range(PASSES):
-                    raw = keep.tile([P, PACK, N], F32, name=f"w_raw{e}{a}", tag=f"w_raw{e}{a}")
-                    nc.sync.dma_start(out=raw[:].rearrange("p j n -> p (j n)"), in_=w_view[:, e, a])
-                    halves.append(raw)
-                w_raw.append(halves)
+        whole_raw = []
+        for e in range(WHOLE):
+            raw = keep.tile([P, PASSES, PACK, N], F32, name=f"whole_raw{e}", tag=f"whole_raw{e}", align_bytes=64)
+            nc.sync.dma_start(out=raw[:].rearrange("p a j n -> p a (j n)"), in_=w_view[:, e])
+            whole_raw.append(raw)
+        pass_raw = {}
+        for e in range(WHOLE, E):
+            for a in range(PASSES):
+                raw = keep.tile([P, PACK, N], F32, name=f"pass_raw{e}{a}", tag=f"pass_raw{e}{a}", align_bytes=64)
+                nc.sync.dma_start(out=raw[:].rearrange("p j n -> p (j n)"), in_=w_view[:, e, a])
+                pass_raw[e, a] = raw
         nc.sync.dma_start(bias[:], b)
         nc.sync.dma_start(pos1_t[:], pos1)
         nc.sync.dma_start(gate1[:], gate[0])
         nc.sync.dma_start(pos2_t[:], pos2)
         nc.sync.dma_start(gate2[:], gate[1])
 
-        def quantize_tokens(a, h, grouped):
+        def quantize_tokens(a, h, staged):
             cols = slice(h * HALF, (h + 1) * HALF)
             nc.vector.quantize_mx(
                 out=x_words[a][:, cols].bitcast(FP8X4),
-                scales=x_scales[4 * a : P, cols],
-                in_=grouped[:].rearrange("p w t -> p (w t)"),
+                scales=x_scales[PLANE_STEP * a : P, cols],
+                in_=staged[:].rearrange("p t j -> p (t j)"),
             )
 
         def gather_words(a):
-            gathered = keep.tile([P, E * C], U32, name=f"g_words{a}", align_bytes=64)
+            gathered = keep.tile([P, SLOTS], U32, name=f"slot_words{a}", align_bytes=64)
             nc.vector.tensor_copy(out=gathered[:], in_=x_words[a][:].bitcast(U32).indirect(offs_t[:]))
             return gathered
 
-        g_words = []
-        x0_grouped = [keep.tile([P, HALF, PACK], BF16, name=f"x0_grouped{h}", align_bytes=64) for h in range(2)]
-        interleave(nc.scalar.copy, x0_grouped[0][:, 0:X0_SCALAR], x0_raw[:, :, 0:X0_SCALAR])
-        interleave(nc.vector.tensor_copy, x0_grouped[1][:], x0_raw[:, :, HALF:T])
-        interleave(nc.vector.tensor_copy, x0_grouped[0][:, X0_SCALAR:HALF], x0_raw[:, :, X0_SCALAR:HALF])
-        for h in (1, 0):
-            quantize_tokens(0, h, x0_grouped[h])
-        g_words.append(gather_words(0))
-        x1_grouped = [keep.tile([P, HALF, PACK], BF16, name=f"x1_grouped{h}", align_bytes=64) for h in range(2)]
-        split = HALF - X1_VECTOR
-        interleave(nc.scalar.copy, x1_grouped[0][:], x1_raw[:, :, 0:HALF])
-        interleave(nc.scalar.copy, x1_grouped[1][:, 0:split], x1_raw[:, :, HALF : HALF + split])
-        interleave(nc.vector.tensor_copy, x1_grouped[1][:, split:HALF], x1_raw[:, :, HALF + split : T])
-        for h in range(2):
-            quantize_tokens(1, h, x1_grouped[h])
-        g_words.append(gather_words(1))
-
-        def gather_scales(half, tag):
-            gathered = keep.tile([P, E * C // 2], U8, name=f"g_scales{half}", tag=tag, align_bytes=64)
-            cols = slice(half * E * C // 32, (half + 1) * E * C // 32)
-            nc.vector.tensor_copy(out=gathered[:], in_=x_scales[:].indirect(offs_t[:, cols]))
+        def gather_scales(h, tag):
+            gathered = keep.tile([P, SLOTS // 2], U8, name=f"slot_scales{h}", tag=tag, align_bytes=64)
+            columns = SLOTS // 2 // LIST_ROWS
+            nc.vector.tensor_copy(out=gathered[:], in_=x_scales[:].indirect(offs_t[:, h * columns : (h + 1) * columns]))
             return gathered
 
-        g_scales = [gather_scales(0, "g_scales0")]
+        x0_staged = [keep.tile([P, HALF, PACK], BF16, name=f"x0_staged{h}", align_bytes=64) for h in range(2)]
+        interleave(nc.scalar.copy, x0_staged[0][:, 0:PASS0_SCALAR], x0_raw[:, :, 0:PASS0_SCALAR])
+        interleave(nc.vector.tensor_copy, x0_staged[1][:], x0_raw[:, :, HALF:T])
+        interleave(nc.vector.tensor_copy, x0_staged[0][:, PASS0_SCALAR:HALF], x0_raw[:, :, PASS0_SCALAR:HALF])
+        for h in (1, 0):
+            quantize_tokens(0, h, x0_staged[h])
+        slot_words = [gather_words(0)]
 
-        w_grouped = keep.tile([P, E, PASSES, N, PACK], BF16, name="w_grouped", align_bytes=64)
+        x1_staged = [keep.tile([P, HALF, PACK], BF16, name=f"x1_staged{h}", align_bytes=64) for h in range(2)]
+        split = HALF - PASS1_VECTOR
+        interleave(nc.scalar.copy, x1_staged[0][:], x1_raw[:, :, 0:HALF])
+        interleave(nc.scalar.copy, x1_staged[1][:, 0:split], x1_raw[:, :, HALF : HALF + split])
+        interleave(nc.vector.tensor_copy, x1_staged[1][:, split:HALF], x1_raw[:, :, HALF + split : T])
+        for h in range(2):
+            quantize_tokens(1, h, x1_staged[h])
+        slot_words.append(gather_words(1))
+        slot_scales = [gather_scales(0, "slot_scales0")]
+
         w_words = keep.tile([P, E, PASSES, N], U32, name="w_words", align_bytes=64)
         w_scales = keep.tile([P, E, PASSES, N], U8, name="w_scales", align_bytes=64)
         acc = [psum.tile([P, C], F32, name=f"acc{e}") for e in range(E)]
 
-        def quantize_weights(first, count):
-            cols = slice(first * N, (first + count) * N)
+        def quantize_weights(e, a, staged):
+            first = (e * PASSES + a) * N
+            cols = slice(first, first + staged.shape[1] * N)
             nc.vector.quantize_mx(
                 out=w_words[:].rearrange("p e a n -> p (e a n)")[:, cols].bitcast(FP8X4),
                 scales=w_scales[:].rearrange("p e a n -> p (e a n)")[:, cols],
-                in_=w_grouped[:].rearrange("p e a n t -> p (e a n t)")[:, first * N * PACK : (first + count) * N * PACK],
+                in_=staged.rearrange("p a n j -> p (a n j)"),
             )
 
-        def multiply(e):
+        w0_staged = keep.tile([P, PASSES, N, PACK], BF16, name="w0_staged", align_bytes=64)
+        interleave(nc.scalar.copy, w0_staged[:], whole_raw[0][:])
+        w1_staged = keep.tile([P, PASSES, N, PACK], BF16, name="w1_staged", tag="whole_raw0", align_bytes=64)
+        for a in range(PASSES):
+            nc.gpsimd.tensor_scalar(w1_staged[:, a], whole_raw[1][:, a].rearrange("p j n -> p n j"), 1.0, 0.0, MULT, ADD)
+        shared = keep.tile([P, (E - FIRST_SHARED) * PASSES, N, PACK], BF16, name="shared", align_bytes=64)
+
+        def staged_passes(e, a, count):
+            first = (e - FIRST_SHARED) * PASSES + a
+            return shared[:, first : first + count]
+
+        last = (E - 1, PASSES - 1)
+        for e, a in pass_raw:
+            if (e, a) != last:
+                interleave(nc.scalar.copy, staged_passes(e, a, 1)[:, 0], pass_raw[e, a][:])
+        y = keep.tile([P, SLOTS], F32, name="y", tag=f"pass_raw{E - 1}0", align_bytes=64)
+
+        quantize_weights(0, 0, w0_staged[:])
+        quantize_weights(1, 0, w1_staged[:])
+        slot_scales.append(gather_scales(1, f"pass_raw{FIRST_SHARED}1"))
+        for e in range(FIRST_SHARED, E - 2, 2):
+            quantize_weights(e, 0, staged_passes(e, 0, 2 * PASSES))
+        quantize_weights(E - 2, 0, staged_passes(E - 2, 0, PASSES))
+        interleave(nc.vector.tensor_copy, staged_passes(*last, 1)[:, 0], pass_raw[last][:])
+        for a in range(PASSES):
+            quantize_weights(E - 1, a, staged_passes(E - 1, a, 1))
+
+        for e in range(E):
             slots = slice(e * C, (e + 1) * C)
-            own = slice((e % 4) * C, (e % 4 + 1) * C)
+            h, place = divmod(e, E // 2)
             for a in range(PASSES):
                 nc.tensor.matmul_mx(
                     out=acc[e][:],
                     lhsT=w_words[:, e, a, :].bitcast(FP8X4),
                     lhsT_scale=w_scales[:, e, a, :],
-                    rhs=g_words[a][:, slots].bitcast(FP8X4),
-                    rhs_scale=g_scales[e // 4][4 * a : P, own],
+                    rhs=slot_words[a][:, slots].bitcast(FP8X4),
+                    rhs_scale=slot_scales[h][PLANE_STEP * a : P, place * C : (place + 1) * C],
                     start=(a == 0),
                     stop=(a == PASSES - 1),
                 )
-
-        def add_bias(y, e):
-            slots = slice(e * C, (e + 1) * C)
             nc.scalar.activation(y[:, slots], acc[e][:], IDENTITY, bias=bias[:, e : e + 1])
 
-        for e in range(WHOLE):
-            if e == GPSIMD_EXPERT:
-                for a in range(PASSES):
-                    nc.gpsimd.tensor_scalar(
-                        w_grouped[:, e, a], w_raw[e][:, a].rearrange("p t n -> p n t"), 1.0, 0.0, MULT, ADD
-                    )
-            else:
-                interleave(nc.scalar.copy, w_grouped[:, e], w_raw[e][:])
-        for e in range(WHOLE, E):
-            for a in range(PASSES):
-                if (e, a) != (E - 1, PASSES - 1):
-                    interleave(nc.scalar.copy, w_grouped[:, e, a], w_raw[e][a][:])
-        y = keep.tile([P, E * C], F32, name="y", tag=f"w_raw{E - 1}0")
-        quantize_weights(0, 4)
-        g_scales.append(gather_scales(1, "w_raw1"))
-        quantize_weights(4, 4)
-        quantize_weights(8, 4)
-        quantize_weights(12, 2)
-        interleave(nc.vector.tensor_copy, w_grouped[:, E - 1, 1], w_raw[E - 1][1][:])
-        quantize_weights(14, 1)
-        quantize_weights(15, 1)
-        for e in range(E):
-            multiply(e)
-            add_bias(y, e)
-
-        part1 = keep.tile([P, T], F32, name="part1")
-        nc.vector.tensor_tensor(part1[:], y[:].indirect(pos1_t[:]), gate1[:], MULT)
-        pieces = ((0, CUT), (CUT, T))
-        part2 = []
-        for lo, hi in pieces:
-            part = keep.tile([P, hi - lo], F32, name=f"part2_{lo}")
-            nc.vector.tensor_tensor(part[:], y[:].indirect(pos2_t[:, lo // 16 : hi // 16]), gate2[:, lo:hi], MULT)
-            part2.append(part)
-        for (lo, hi), part in zip(pieces, part2):
+        first_part = keep.tile([P, T], F32, name="first_part")
+        nc.vector.tensor_tensor(first_part[:], y[:].indirect(pos1_t[:]), gate1[:], MULT)
+        halves = ((0, HALF), (HALF, T))
+        second_parts = []
+        for lo, hi in halves:
+            part = keep.tile([P, hi - lo], F32, name=f"second_part{lo}")
+            offsets = pos2_t[:, lo // LIST_ROWS : hi // LIST_ROWS]
+            nc.vector.tensor_tensor(part[:], y[:].indirect(offsets), gate2[:, lo:hi], MULT)
+            second_parts.append(part)
+        for (lo, hi), part in zip(halves, second_parts):
             total = keep.tile([P, hi - lo], F32, name=f"total{lo}")
-            nc.vector.tensor_add(total[:], part1[:, lo:hi], part[:])
+            nc.vector.tensor_add(total[:], first_part[:, lo:hi], part[:])
             nc.sync.dma_start(out=out[:, lo:hi], in_=total[:])

@@ -27,6 +27,7 @@ WINDOW = 1376
 PASS0_SCALAR = 176
 PASS1_VECTOR = 64
 WHOLE = 2
+BURST = 256
 FIRST_SHARED = 2
 
 
@@ -49,8 +50,8 @@ def tile_routed_moe_kernel(tc, xT, w, b, gate, offs, pos1, pos2, out):
         pos1_t = keep.tile([P, T // LIST_ROWS], U16, name="pos1_t")
         pos2_t = keep.tile([P, T // LIST_ROWS], U16, name="pos2_t")
         bias = keep.tile([P, E], F32, name="bias")
-        gate1 = keep.tile([P, T], F32, name="gate1")
-        gate2 = keep.tile([P, T], F32, name="gate2")
+        gate1 = keep.tile([P, T], F32, name="gate1", align_bytes=BURST)
+        gate2 = keep.tile([P, T], F32, name="gate2", align_bytes=BURST)
 
         x_scales = keep.tile([P, WINDOW], U8, name="x_scales", align_bytes=64)
         nc.gpsimd.memset(x_scales[:], 0)
@@ -60,20 +61,20 @@ def tile_routed_moe_kernel(tc, xT, w, b, gate, offs, pos1, pos2, out):
             nc.vector.memset(words[:, T:WINDOW], 0)
             x_words.append(words)
 
-        x0_raw = keep.tile([P, PACK, T], F32, name="x0_raw")
+        x0_raw = keep.tile([P, PACK, T], F32, name="x0_raw", align_bytes=BURST)
         nc.sync.dma_start(out=x0_raw[:], in_=x_view[0])
         nc.sync.dma_start(offs_t[:], offs)
-        x1_raw = keep.tile([P, PACK, T], F32, name="x1_raw")
+        x1_raw = keep.tile([P, PACK, T], F32, name="x1_raw", align_bytes=BURST)
         nc.sync.dma_start(out=x1_raw[:], in_=x_view[1])
         whole_raw = []
         for e in range(WHOLE):
-            raw = keep.tile([P, PASSES, PACK, N], F32, name=f"whole_raw{e}", tag=f"whole_raw{e}", align_bytes=64)
+            raw = keep.tile([P, PASSES, PACK, N], F32, name=f"whole_raw{e}", tag=f"whole_raw{e}", align_bytes=BURST)
             nc.sync.dma_start(out=raw[:].rearrange("p a j n -> p a (j n)"), in_=w_view[:, e])
             whole_raw.append(raw)
         pass_raw = {}
         for e in range(WHOLE, E):
             for a in range(PASSES):
-                raw = keep.tile([P, PACK, N], F32, name=f"pass_raw{e}{a}", tag=f"pass_raw{e}{a}", align_bytes=64)
+                raw = keep.tile([P, PACK, N], F32, name=f"pass_raw{e}{a}", tag=f"pass_raw{e}{a}", align_bytes=BURST)
                 nc.sync.dma_start(out=raw[:].rearrange("p j n -> p (j n)"), in_=w_view[:, e, a])
                 pass_raw[e, a] = raw
         nc.sync.dma_start(bias[:], b)
@@ -96,7 +97,7 @@ def tile_routed_moe_kernel(tc, xT, w, b, gate, offs, pos1, pos2, out):
             return gathered
 
         def gather_scales(h, tag):
-            gathered = keep.tile([P, SLOTS // 2], U8, name=f"slot_scales{h}", tag=tag, align_bytes=64)
+            gathered = keep.tile([P, SLOTS // 2], U8, name=f"slot_scales{h}", tag=tag, align_bytes=BURST)
             columns = SLOTS // 2 // LIST_ROWS
             nc.vector.tensor_copy(out=gathered[:], in_=x_scales[:].indirect(offs_t[:, h * columns : (h + 1) * columns]))
             return gathered
@@ -134,7 +135,7 @@ def tile_routed_moe_kernel(tc, xT, w, b, gate, offs, pos1, pos2, out):
 
         w0_staged = keep.tile([P, PASSES, N, PACK], BF16, name="w0_staged", align_bytes=64)
         interleave(nc.scalar.copy, w0_staged[:], whole_raw[0][:])
-        w1_staged = keep.tile([P, PASSES, N, PACK], BF16, name="w1_staged", tag="whole_raw0", align_bytes=64)
+        w1_staged = keep.tile([P, PASSES, N, PACK], BF16, name="w1_staged", tag="whole_raw0", align_bytes=BURST)
         for a in range(PASSES):
             nc.gpsimd.tensor_scalar(w1_staged[:, a], whole_raw[1][:, a].rearrange("p j n -> p n j"), 1.0, 0.0, MULT, ADD)
         shared = keep.tile([P, (E - FIRST_SHARED) * PASSES, N, PACK], BF16, name="shared", align_bytes=64)
@@ -147,7 +148,7 @@ def tile_routed_moe_kernel(tc, xT, w, b, gate, offs, pos1, pos2, out):
         for e, a in pass_raw:
             if (e, a) != last:
                 interleave(nc.scalar.copy, staged_passes(e, a, 1)[:, 0], pass_raw[e, a][:])
-        y = keep.tile([P, SLOTS], F32, name="y", tag=f"pass_raw{E - 1}0", align_bytes=64)
+        y = keep.tile([P, SLOTS], F32, name="y", tag=f"pass_raw{E - 1}0", align_bytes=BURST)
 
         quantize_weights(0, 0, w0_staged[:])
         quantize_weights(1, 0, w1_staged[:])
@@ -184,6 +185,6 @@ def tile_routed_moe_kernel(tc, xT, w, b, gate, offs, pos1, pos2, out):
             nc.vector.tensor_tensor(part[:], y[:].indirect(offsets), gate2[:, lo:hi], MULT)
             second_parts.append(part)
         for (lo, hi), part in zip(halves, second_parts):
-            total = keep.tile([P, hi - lo], F32, name=f"total{lo}")
+            total = keep.tile([P, hi - lo], F32, name=f"total{lo}", align_bytes=BURST)
             nc.vector.tensor_add(total[:], first_part[:, lo:hi], part[:])
             nc.sync.dma_start(out=out[:, lo:hi], in_=total[:])

@@ -24,8 +24,8 @@ LIST_ROWS = 16
 PLANE_STEP = 4
 HALF = T // 2
 WINDOW = 1376
-PASS0_SCALAR = 176
-PASS1_VECTOR = 64
+PASS0_SCALAR = 96
+PASS1_VECTOR = 32
 WHOLE = 2
 BURST = 256
 FIRST_SHARED = 2
@@ -61,11 +61,13 @@ def tile_routed_moe_kernel(tc, xT, w, b, gate, offs, pos1, pos2, out):
             nc.vector.memset(words[:, T:WINDOW], 0)
             x_words.append(words)
 
-        x0_raw = keep.tile([P, PACK, T], F32, name="x0_raw", align_bytes=BURST)
-        nc.sync.dma_start(out=x0_raw[:], in_=x_view[0])
-        nc.sync.dma_start(offs_t[:], offs)
-        x1_raw = keep.tile([P, PACK, T], F32, name="x1_raw", align_bytes=BURST)
-        nc.sync.dma_start(out=x1_raw[:], in_=x_view[1])
+        x_raw = {}
+        for a in range(PASSES):
+            for h in range(2):
+                x_raw[a, h] = keep.tile([P, PACK, HALF], F32, name=f"x_raw{a}{h}", align_bytes=BURST)
+                nc.sync.dma_start(out=x_raw[a, h][:], in_=x_view[a][:, :, h * HALF : (h + 1) * HALF])
+            if a == 0:
+                nc.sync.dma_start(offs_t[:], offs)
         whole_raw = []
         for e in range(WHOLE):
             raw = keep.tile([P, PASSES, PACK, N], F32, name=f"whole_raw{e}", tag=f"whole_raw{e}", align_bytes=BURST)
@@ -103,18 +105,17 @@ def tile_routed_moe_kernel(tc, xT, w, b, gate, offs, pos1, pos2, out):
             return gathered
 
         x0_staged = [keep.tile([P, HALF, PACK], BF16, name=f"x0_staged{h}", align_bytes=64) for h in range(2)]
-        interleave(nc.scalar.copy, x0_staged[0][:, 0:PASS0_SCALAR], x0_raw[:, :, 0:PASS0_SCALAR])
-        interleave(nc.vector.tensor_copy, x0_staged[1][:], x0_raw[:, :, HALF:T])
-        interleave(nc.vector.tensor_copy, x0_staged[0][:, PASS0_SCALAR:HALF], x0_raw[:, :, PASS0_SCALAR:HALF])
-        for h in (1, 0):
+        for h in range(2):
+            interleave(nc.scalar.copy, x0_staged[h][:, 0:PASS0_SCALAR], x_raw[0, h][:, :, 0:PASS0_SCALAR])
+            interleave(nc.vector.tensor_copy, x0_staged[h][:, PASS0_SCALAR:HALF], x_raw[0, h][:, :, PASS0_SCALAR:HALF])
             quantize_tokens(0, h, x0_staged[h])
         slot_words = [gather_words(0)]
 
         x1_staged = [keep.tile([P, HALF, PACK], BF16, name=f"x1_staged{h}", align_bytes=64) for h in range(2)]
         split = HALF - PASS1_VECTOR
-        interleave(nc.scalar.copy, x1_staged[0][:], x1_raw[:, :, 0:HALF])
-        interleave(nc.scalar.copy, x1_staged[1][:, 0:split], x1_raw[:, :, HALF : HALF + split])
-        interleave(nc.vector.tensor_copy, x1_staged[1][:, split:HALF], x1_raw[:, :, HALF + split : T])
+        interleave(nc.scalar.copy, x1_staged[0][:], x_raw[1, 0][:])
+        interleave(nc.scalar.copy, x1_staged[1][:, 0:split], x_raw[1, 1][:, :, 0:split])
+        interleave(nc.vector.tensor_copy, x1_staged[1][:, split:HALF], x_raw[1, 1][:, :, split:HALF])
         for h in range(2):
             quantize_tokens(1, h, x1_staged[h])
         slot_words.append(gather_words(1))

@@ -26,7 +26,8 @@ HALF = T // 2
 WINDOW = 1376
 PASS0_SCALAR = 96
 PASS1_VECTOR = 32
-WHOLE = 2
+W_LOADS = [(0, 3), (3, 2)] + [(s, 1) for s in range(5, E * PASSES)]
+GPSIMD_LOAD = 3
 BURST = 256
 FIRST_SHARED = 2
 
@@ -34,7 +35,7 @@ FIRST_SHARED = 2
 def tile_routed_moe_kernel(tc, xT, w, b, gate, offs, pos1, pos2, out):
     nc = tc.nc
     x_view = xT.rearrange("(a p j) t -> a p j t", p=P, j=PACK)
-    w_view = w.rearrange("e (a p j) n -> p e a (j n)", p=P, j=PACK)
+    w_view = w.rearrange("e (a p j) n -> p (e a) (j n)", p=P, j=PACK)
 
     def interleave(copy, dst, src):
         if len(src.shape) == 3:
@@ -50,8 +51,7 @@ def tile_routed_moe_kernel(tc, xT, w, b, gate, offs, pos1, pos2, out):
         pos1_t = keep.tile([P, T // LIST_ROWS], U16, name="pos1_t")
         pos2_t = keep.tile([P, T // LIST_ROWS], U16, name="pos2_t")
         bias = keep.tile([P, E], F32, name="bias")
-        gate1 = keep.tile([P, T], F32, name="gate1", align_bytes=BURST)
-        gate2 = keep.tile([P, T], F32, name="gate2", align_bytes=BURST)
+        gates = keep.tile([P, 2, T], F32, name="gates", align_bytes=BURST)
 
         x_scales = keep.tile([P, WINDOW], U8, name="x_scales", align_bytes=64)
         nc.gpsimd.memset(x_scales[:], 0)
@@ -68,22 +68,15 @@ def tile_routed_moe_kernel(tc, xT, w, b, gate, offs, pos1, pos2, out):
                 nc.sync.dma_start(out=x_raw[a, h][:], in_=x_view[a][:, :, h * HALF : (h + 1) * HALF])
             if a == 0:
                 nc.sync.dma_start(offs_t[:], offs)
-        whole_raw = []
-        for e in range(WHOLE):
-            raw = keep.tile([P, PASSES, PACK, N], F32, name=f"whole_raw{e}", tag=f"whole_raw{e}", align_bytes=BURST)
-            nc.sync.dma_start(out=raw[:].rearrange("p a j n -> p a (j n)"), in_=w_view[:, e])
-            whole_raw.append(raw)
-        pass_raw = {}
-        for e in range(WHOLE, E):
-            for a in range(PASSES):
-                raw = keep.tile([P, PACK, N], F32, name=f"pass_raw{e}{a}", tag=f"pass_raw{e}{a}", align_bytes=BURST)
-                nc.sync.dma_start(out=raw[:].rearrange("p j n -> p (j n)"), in_=w_view[:, e, a])
-                pass_raw[e, a] = raw
+        w_raw = []
+        for first, count in W_LOADS:
+            raw = keep.tile([P, count, PACK, N], F32, name=f"w_raw{first}", tag=f"w_raw{first}", align_bytes=BURST)
+            nc.sync.dma_start(out=raw[:].rearrange("p s j n -> p s (j n)"), in_=w_view[:, first : first + count])
+            w_raw.append(raw)
         nc.sync.dma_start(bias[:], b)
         nc.sync.dma_start(pos1_t[:], pos1)
-        nc.sync.dma_start(gate1[:], gate[0])
+        nc.sync.dma_start(gates[:], gate.rearrange("r p t -> p r t"))
         nc.sync.dma_start(pos2_t[:], pos2)
-        nc.sync.dma_start(gate2[:], gate[1])
 
         def quantize_tokens(a, h, staged):
             cols = slice(h * HALF, (h + 1) * HALF)
@@ -112,11 +105,8 @@ def tile_routed_moe_kernel(tc, xT, w, b, gate, offs, pos1, pos2, out):
         slot_words = [gather_words(0)]
 
         x1_staged = [keep.tile([P, HALF, PACK], BF16, name=f"x1_staged{h}", align_bytes=64) for h in range(2)]
-        split = HALF - PASS1_VECTOR
-        interleave(nc.scalar.copy, x1_staged[0][:], x_raw[1, 0][:])
-        interleave(nc.scalar.copy, x1_staged[1][:, 0:split], x_raw[1, 1][:, :, 0:split])
-        interleave(nc.vector.tensor_copy, x1_staged[1][:, split:HALF], x_raw[1, 1][:, :, split:HALF])
         for h in range(2):
+            interleave(nc.scalar.copy, x1_staged[h][:], x_raw[1, h][:])
             quantize_tokens(1, h, x1_staged[h])
         slot_words.append(gather_words(1))
         slot_scales = [gather_scales(0, "slot_scales0")]
@@ -134,30 +124,27 @@ def tile_routed_moe_kernel(tc, xT, w, b, gate, offs, pos1, pos2, out):
                 in_=staged.rearrange("p a n j -> p (a n j)"),
             )
 
-        w0_staged = keep.tile([P, PASSES, N, PACK], BF16, name="w0_staged", align_bytes=64)
-        interleave(nc.scalar.copy, w0_staged[:], whole_raw[0][:])
-        w1_staged = keep.tile([P, PASSES, N, PACK], BF16, name="w1_staged", tag="whole_raw0", align_bytes=BURST)
-        for a in range(PASSES):
-            nc.gpsimd.tensor_scalar(w1_staged[:, a], whole_raw[1][:, a].rearrange("p j n -> p n j"), 1.0, 0.0, MULT, ADD)
-        shared = keep.tile([P, (E - FIRST_SHARED) * PASSES, N, PACK], BF16, name="shared", align_bytes=64)
+        staged = keep.tile([P, E * PASSES, N, PACK], BF16, name="staged", align_bytes=64)
 
         def staged_passes(e, a, count):
-            first = (e - FIRST_SHARED) * PASSES + a
-            return shared[:, first : first + count]
+            first = e * PASSES + a
+            return staged[:, first : first + count]
 
-        last = (E - 1, PASSES - 1)
-        for e, a in pass_raw:
-            if (e, a) != last:
-                interleave(nc.scalar.copy, staged_passes(e, a, 1)[:, 0], pass_raw[e, a][:])
-        y = keep.tile([P, SLOTS], F32, name="y", tag=f"pass_raw{E - 1}0", align_bytes=BURST)
+        for (first, count), raw in zip(W_LOADS[:-1], w_raw):
+            if first == GPSIMD_LOAD:
+                for s in range(count):
+                    nc.gpsimd.tensor_scalar(staged[:, first + s], raw[:, s].rearrange("p j n -> p n j"), 1.0, 0.0, MULT, ADD)
+            else:
+                for s in range(count):
+                    interleave(nc.scalar.copy, staged[:, first + s], raw[:, s])
+        y = keep.tile([P, SLOTS], F32, name="y", tag=f"w_raw{W_LOADS[-2][0]}", align_bytes=BURST)
 
-        quantize_weights(0, 0, w0_staged[:])
-        quantize_weights(1, 0, w1_staged[:])
-        slot_scales.append(gather_scales(1, f"pass_raw{FIRST_SHARED}1"))
+        quantize_weights(0, 0, staged_passes(0, 0, 2 * PASSES))
+        slot_scales.append(gather_scales(1, "w_raw5"))
         for e in range(FIRST_SHARED, E - 2, 2):
             quantize_weights(e, 0, staged_passes(e, 0, 2 * PASSES))
         quantize_weights(E - 2, 0, staged_passes(E - 2, 0, PASSES))
-        interleave(nc.vector.tensor_copy, staged_passes(*last, 1)[:, 0], pass_raw[last][:])
+        interleave(nc.vector.tensor_copy, staged[:, E * PASSES - 1], w_raw[-1][:, 0])
         for a in range(PASSES):
             quantize_weights(E - 1, a, staged_passes(E - 1, a, 1))
 
@@ -177,13 +164,13 @@ def tile_routed_moe_kernel(tc, xT, w, b, gate, offs, pos1, pos2, out):
             nc.scalar.activation(y[:, slots], acc[e][:], IDENTITY, bias=bias[:, e : e + 1])
 
         first_part = keep.tile([P, T], F32, name="first_part")
-        nc.vector.tensor_tensor(first_part[:], y[:].indirect(pos1_t[:]), gate1[:], MULT)
+        nc.vector.tensor_tensor(first_part[:], y[:].indirect(pos1_t[:]), gates[:, 0], MULT)
         halves = ((0, HALF), (HALF, T))
         second_parts = []
         for lo, hi in halves:
             part = keep.tile([P, hi - lo], F32, name=f"second_part{lo}")
             offsets = pos2_t[:, lo // LIST_ROWS : hi // LIST_ROWS]
-            nc.vector.tensor_tensor(part[:], y[:].indirect(offsets), gate2[:, lo:hi], MULT)
+            nc.vector.tensor_tensor(part[:], y[:].indirect(offsets), gates[:, 1, lo:hi], MULT)
             second_parts.append(part)
         for (lo, hi), part in zip(halves, second_parts):
             total = keep.tile([P, hi - lo], F32, name=f"total{lo}", align_bytes=BURST)

@@ -29,6 +29,7 @@ PASS1_VECTOR = 32
 W_LOADS = [(0, 3), (3, 2)] + [(s, 1) for s in range(5, E * PASSES)]
 GPSIMD_LOAD = 3
 BURST = 256
+JOINT = range(5, 7)
 FIRST_SHARED = 2
 
 
@@ -47,10 +48,10 @@ def tile_routed_moe_kernel(tc, xT, w, b, gate, offs, pos1, pos2, out):
         keep = ctx.enter_context(tc.tile_pool(name="keep", bufs=1))
         psum = ctx.enter_context(tc.psum_pool(name="psum", bufs=1))
 
-        offs_t = keep.tile([P, SLOTS // LIST_ROWS], U16, name="offs_t")
-        pos1_t = keep.tile([P, T // LIST_ROWS], U16, name="pos1_t")
-        pos2_t = keep.tile([P, T // LIST_ROWS], U16, name="pos2_t")
-        bias = keep.tile([P, E], F32, name="bias")
+        offs_t = keep.tile([P, SLOTS // LIST_ROWS], U16, name="offs_t", align_bytes=BURST)
+        pos1_t = keep.tile([P, T // LIST_ROWS], U16, name="pos1_t", align_bytes=BURST)
+        pos2_t = keep.tile([P, T // LIST_ROWS], U16, name="pos2_t", align_bytes=BURST)
+        bias = keep.tile([P, E], F32, name="bias", align_bytes=BURST)
         gates = keep.tile([P, 2, T], F32, name="gates", align_bytes=BURST)
 
         x_scales = keep.tile([P, WINDOW], U8, name="x_scales", align_bytes=64)
@@ -113,7 +114,8 @@ def tile_routed_moe_kernel(tc, xT, w, b, gate, offs, pos1, pos2, out):
 
         w_words = keep.tile([P, E, PASSES, N], U32, name="w_words", align_bytes=64)
         w_scales = keep.tile([P, E, PASSES, N], U8, name="w_scales", align_bytes=64)
-        acc = [psum.tile([P, C], F32, name=f"acc{e}") for e in range(E)]
+        joint = psum.tile([P, len(JOINT), C], F32, name="joint")
+        acc = [joint[:, e - JOINT.start] if e in JOINT else psum.tile([P, C], F32, name=f"acc{e}")[:] for e in range(E)]
 
         def quantize_weights(e, a, staged):
             first = (e * PASSES + a) * N
@@ -140,8 +142,9 @@ def tile_routed_moe_kernel(tc, xT, w, b, gate, offs, pos1, pos2, out):
         y = keep.tile([P, SLOTS], F32, name="y", tag=f"w_raw{W_LOADS[-2][0]}", align_bytes=BURST)
 
         quantize_weights(0, 0, staged_passes(0, 0, 2 * PASSES))
-        slot_scales.append(gather_scales(1, "w_raw5"))
-        for e in range(FIRST_SHARED, E - 2, 2):
+        quantize_weights(2, 0, staged_passes(2, 0, 2 * PASSES))
+        slot_scales.append(gather_scales(1, "w_raw7"))
+        for e in range(4, E - 2, 2):
             quantize_weights(e, 0, staged_passes(e, 0, 2 * PASSES))
         quantize_weights(E - 2, 0, staged_passes(E - 2, 0, PASSES))
         interleave(nc.vector.tensor_copy, staged[:, E * PASSES - 1], w_raw[-1][:, 0])
@@ -153,7 +156,7 @@ def tile_routed_moe_kernel(tc, xT, w, b, gate, offs, pos1, pos2, out):
             h, place = divmod(e, E // 2)
             for a in range(PASSES):
                 nc.tensor.matmul_mx(
-                    out=acc[e][:],
+                    out=acc[e],
                     lhsT=w_words[:, e, a, :].bitcast(FP8X4),
                     lhsT_scale=w_scales[:, e, a, :],
                     rhs=slot_words[a][:, slots].bitcast(FP8X4),
@@ -161,7 +164,14 @@ def tile_routed_moe_kernel(tc, xT, w, b, gate, offs, pos1, pos2, out):
                     start=(a == 0),
                     stop=(a == PASSES - 1),
                 )
-            nc.scalar.activation(y[:, slots], acc[e][:], IDENTITY, bias=bias[:, e : e + 1])
+            if e not in JOINT:
+                nc.scalar.activation(y[:, slots], acc[e], IDENTITY, bias=bias[:, e : e + 1])
+        nc.vector.tensor_tensor(
+            y[:, JOINT.start * C : JOINT.stop * C].rearrange("p (e c) -> p e c", c=C),
+            joint[:],
+            bias[:, JOINT.start : JOINT.stop].unsqueeze(2).to_broadcast([P, len(JOINT), C]),
+            ADD,
+        )
 
         first_part = keep.tile([P, T], F32, name="first_part")
         nc.vector.tensor_tensor(first_part[:], y[:].indirect(pos1_t[:]), gates[:, 0], MULT)

@@ -25,12 +25,11 @@ PLANE_STEP = 4
 HALF = T // 2
 WINDOW = 1376
 PASS0_SCALAR = 96
-PASS1_VECTOR = 32
+LAST_SCALAR = 64
 W_LOADS = [(0, 3), (3, 2)] + [(s, 1) for s in range(5, E * PASSES)]
 GPSIMD_LOAD = 3
 BURST = 256
-JOINT = range(5, 7)
-FIRST_SHARED = 2
+JOINT = range(4, 7)
 
 
 def tile_routed_moe_kernel(tc, xT, w, b, gate, offs, pos1, pos2, out):
@@ -139,7 +138,8 @@ def tile_routed_moe_kernel(tc, xT, w, b, gate, offs, pos1, pos2, out):
             else:
                 for s in range(count):
                     interleave(nc.scalar.copy, staged[:, first + s], raw[:, s])
-        y = keep.tile([P, SLOTS], F32, name="y", tag=f"w_raw{W_LOADS[-2][0]}", align_bytes=BURST)
+        last = E * PASSES - 1
+        interleave(nc.scalar.copy, staged[:, last, 0:LAST_SCALAR], w_raw[-1][:, 0, :, 0:LAST_SCALAR])
 
         quantize_weights(0, 0, staged_passes(0, 0, 2 * PASSES))
         quantize_weights(2, 0, staged_passes(2, 0, 2 * PASSES))
@@ -147,7 +147,8 @@ def tile_routed_moe_kernel(tc, xT, w, b, gate, offs, pos1, pos2, out):
         for e in range(4, E - 2, 2):
             quantize_weights(e, 0, staged_passes(e, 0, 2 * PASSES))
         quantize_weights(E - 2, 0, staged_passes(E - 2, 0, PASSES))
-        interleave(nc.vector.tensor_copy, staged[:, E * PASSES - 1], w_raw[-1][:, 0])
+        interleave(nc.vector.tensor_copy, staged[:, last, LAST_SCALAR:N], w_raw[-1][:, 0, :, LAST_SCALAR:N])
+        y = keep.tile([P, SLOTS], F32, name="y", tag=f"w_raw{last}", align_bytes=BURST)
         for a in range(PASSES):
             quantize_weights(E - 1, a, staged_passes(E - 1, a, 1))
 

@@ -26,8 +26,9 @@ HALF = T // 2
 WINDOW = 1376
 PASS0_SCALAR = 96
 LAST_SCALAR = 64
-W_LOADS = [(0, 3), (3, 2)] + [(s, 1) for s in range(5, E * PASSES)]
-GPSIMD_LOAD = 3
+W_LOADS = [(0, 2), (2, 2), (4, 2)] + [(s, 1) for s in range(6, E * PASSES)]
+GPSIMD_STEPS = (3, 4)
+GROUPS = [(2, 3, 4, 5), (0, 1, 6, 7), (8, 9, 10, 11), (12, 13), (14,), (15,)]
 BURST = 256
 JOINT = range(4, 7)
 
@@ -72,7 +73,7 @@ def tile_routed_moe_kernel(tc, xT, w, b, gate, offs, pos1, pos2, out):
         for first, count in W_LOADS:
             raw = keep.tile([P, count, PACK, N], F32, name=f"w_raw{first}", tag=f"w_raw{first}", align_bytes=BURST)
             nc.sync.dma_start(out=raw[:].rearrange("p s j n -> p s (j n)"), in_=w_view[:, first : first + count])
-            w_raw.append(raw)
+            w_raw.extend(raw[:, s] for s in range(count))
         nc.sync.dma_start(bias[:], b)
         nc.sync.dma_start(pos1_t[:], pos1)
         nc.sync.dma_start(gates[:], gate.rearrange("r p t -> p r t"))
@@ -111,62 +112,66 @@ def tile_routed_moe_kernel(tc, xT, w, b, gate, offs, pos1, pos2, out):
         slot_words.append(gather_words(1))
         slot_scales = [gather_scales(0, "slot_scales0")]
 
-        w_words = keep.tile([P, E, PASSES, N], U32, name="w_words", align_bytes=64)
-        w_scales = keep.tile([P, E, PASSES, N], U8, name="w_scales", align_bytes=64)
+        w_words = keep.tile([P, E * PASSES * N], U32, name="w_words", align_bytes=64)
+        w_scales = keep.tile([P, E * PASSES * N], U8, name="w_scales", align_bytes=64)
+        place = {s: i for i, s in enumerate(s for group in GROUPS for s in group)}
         joint = psum.tile([P, len(JOINT), C], F32, name="joint")
         acc = [joint[:, e - JOINT.start] if e in JOINT else psum.tile([P, C], F32, name=f"acc{e}")[:] for e in range(E)]
+        last = E * PASSES - 1
 
-        def quantize_weights(e, a, staged):
-            first = (e * PASSES + a) * N
-            cols = slice(first, first + staged.shape[1] * N)
+        staged = {}
+
+        def stage(s):
+            g = [s in group for group in GROUPS].index(True)
+            if g not in staged:
+                tag = "w_raw0" if g == 0 else f"staged{g}"
+                staged[g] = keep.tile([P, len(GROUPS[g]), N, PACK], BF16, name=f"staged{g}", tag=tag, align_bytes=BURST)
+            dst = staged[g][:, GROUPS[g].index(s)]
+            if s in GPSIMD_STEPS:
+                nc.gpsimd.tensor_scalar(dst, w_raw[s].rearrange("p j n -> p n j"), 1.0, 0.0, MULT, ADD)
+            elif s == last:
+                interleave(nc.scalar.copy, dst[:, 0:LAST_SCALAR], w_raw[s][:, :, 0:LAST_SCALAR])
+            else:
+                interleave(nc.scalar.copy, dst, w_raw[s])
+
+        def quantize_weights(g, staged):
+            first = place[GROUPS[g][0]] * N
+            cols = slice(first, first + len(GROUPS[g]) * N)
             nc.vector.quantize_mx(
-                out=w_words[:].rearrange("p e a n -> p (e a n)")[:, cols].bitcast(FP8X4),
-                scales=w_scales[:].rearrange("p e a n -> p (e a n)")[:, cols],
-                in_=staged.rearrange("p a n j -> p (a n j)"),
+                out=w_words[:, cols].bitcast(FP8X4),
+                scales=w_scales[:, cols],
+                in_=staged[:].rearrange("p a n j -> p (a n j)"),
             )
 
-        staged = keep.tile([P, E * PASSES, N, PACK], BF16, name="staged", align_bytes=64)
-
-        def staged_passes(e, a, count):
-            first = e * PASSES + a
-            return staged[:, first : first + count]
-
-        for (first, count), raw in zip(W_LOADS[:-1], w_raw):
-            if first == GPSIMD_LOAD:
-                for s in range(count):
-                    nc.gpsimd.tensor_scalar(staged[:, first + s], raw[:, s].rearrange("p j n -> p n j"), 1.0, 0.0, MULT, ADD)
-            else:
-                for s in range(count):
-                    interleave(nc.scalar.copy, staged[:, first + s], raw[:, s])
-        last = E * PASSES - 1
-        interleave(nc.scalar.copy, staged[:, last, 0:LAST_SCALAR], w_raw[-1][:, 0, :, 0:LAST_SCALAR])
-
-        quantize_weights(0, 0, staged_passes(0, 0, 2 * PASSES))
-        quantize_weights(2, 0, staged_passes(2, 0, 2 * PASSES))
+        for s in range(E * PASSES):
+            stage(s)
+        quantize_weights(0, staged[0])
+        quantize_weights(1, staged[1])
         slot_scales.append(gather_scales(1, "w_raw7"))
-        for e in range(4, E - 2, 2):
-            quantize_weights(e, 0, staged_passes(e, 0, 2 * PASSES))
-        quantize_weights(E - 2, 0, staged_passes(E - 2, 0, PASSES))
-        interleave(nc.vector.tensor_copy, staged[:, last, LAST_SCALAR:N], w_raw[-1][:, 0, :, LAST_SCALAR:N])
+        quantize_weights(2, staged[2])
+        quantize_weights(3, staged[3])
+        interleave(nc.vector.tensor_copy, staged[5][:, 0, LAST_SCALAR:N], w_raw[last][:, :, LAST_SCALAR:N])
         y = keep.tile([P, SLOTS], F32, name="y", tag=f"w_raw{last}", align_bytes=BURST)
-        for a in range(PASSES):
-            quantize_weights(E - 1, a, staged_passes(E - 1, a, 1))
+        quantize_weights(4, staged[4])
+        quantize_weights(5, staged[5])
 
-        for e in range(E):
+        for s in sorted(place, key=place.get):
+            e, a = divmod(s, PASSES)
             slots = slice(e * C, (e + 1) * C)
-            h, place = divmod(e, E // 2)
-            for a in range(PASSES):
-                nc.tensor.matmul_mx(
-                    out=acc[e],
-                    lhsT=w_words[:, e, a, :].bitcast(FP8X4),
-                    lhsT_scale=w_scales[:, e, a, :],
-                    rhs=slot_words[a][:, slots].bitcast(FP8X4),
-                    rhs_scale=slot_scales[h][PLANE_STEP * a : P, place * C : (place + 1) * C],
-                    start=(a == 0),
-                    stop=(a == PASSES - 1),
-                )
+            h, at = divmod(e, E // 2)
+            cols = slice(place[s] * N, (place[s] + 1) * N)
+            nc.tensor.matmul_mx(
+                out=acc[e],
+                lhsT=w_words[:, cols].bitcast(FP8X4),
+                lhsT_scale=w_scales[:, cols],
+                rhs=slot_words[a][:, slots].bitcast(FP8X4),
+                rhs_scale=slot_scales[h][PLANE_STEP * a : P, at * C : (at + 1) * C],
+                start=(a == 0),
+                stop=(a == PASSES - 1),
+            )
+        for e in range(E):
             if e not in JOINT:
-                nc.scalar.activation(y[:, slots], acc[e], IDENTITY, bias=bias[:, e : e + 1])
+                nc.scalar.activation(y[:, e * C : (e + 1) * C], acc[e], IDENTITY, bias=bias[:, e : e + 1])
         nc.vector.tensor_tensor(
             y[:, JOINT.start * C : JOINT.stop * C].rearrange("p (e c) -> p e c", c=C),
             joint[:],

@@ -26,8 +26,9 @@ HALF = T // 2
 WINDOW = 1376
 PASS0_SCALAR = 96
 LAST_SCALAR = 64
-W_LOADS = [(0, 2), (2, 2), (4, 2)] + [(s, 1) for s in range(6, E * PASSES)]
+W_LOADS = [(0, 2), (2, 3)] + [(s, 1) for s in range(5, E * PASSES)]
 GPSIMD_STEPS = (3, 4)
+PASS1_GPSIMD = 112
 GROUPS = [(2, 3, 4, 5), (0, 1, 6, 7), (8, 9, 10, 11), (12, 13), (14,), (15,)]
 BURST = 256
 JOINT = range(4, 7)
@@ -65,7 +66,7 @@ def tile_routed_moe_kernel(tc, xT, w, b, gate, offs, pos1, pos2, out):
         x_raw = {}
         for a in range(PASSES):
             for h in range(2):
-                x_raw[a, h] = keep.tile([P, PACK, HALF], F32, name=f"x_raw{a}{h}", align_bytes=BURST)
+                x_raw[a, h] = keep.tile([P, PACK, HALF], F32, name=f"x_raw{a}{h}", tag=f"x_raw{a}{h}", align_bytes=BURST)
                 nc.sync.dma_start(out=x_raw[a, h][:], in_=x_view[a][:, :, h * HALF : (h + 1) * HALF])
             if a == 0:
                 nc.sync.dma_start(offs_t[:], offs)
@@ -87,10 +88,11 @@ def tile_routed_moe_kernel(tc, xT, w, b, gate, offs, pos1, pos2, out):
                 in_=staged[:].rearrange("p t j -> p (t j)"),
             )
 
-        def gather_words(a):
-            gathered = keep.tile([P, SLOTS], U32, name=f"slot_words{a}", align_bytes=64)
-            nc.vector.tensor_copy(out=gathered[:], in_=x_words[a][:].bitcast(U32).indirect(offs_t[:]))
-            return gathered
+        slot_words = [keep.tile([P, SLOTS - C * (1 - a)], U32, name=f"slot_words{a}", align_bytes=64) for a in range(PASSES)]
+
+        def gather_words(dst, a, lo, hi, window):
+            offsets = offs_t[:, lo // LIST_ROWS : hi // LIST_ROWS]
+            nc.vector.tensor_copy(out=dst, in_=x_words[a][:, 0:window].bitcast(U32).indirect(offsets))
 
         def gather_scales(h, tag):
             gathered = keep.tile([P, SLOTS // 2], U8, name=f"slot_scales{h}", tag=tag, align_bytes=BURST)
@@ -103,13 +105,18 @@ def tile_routed_moe_kernel(tc, xT, w, b, gate, offs, pos1, pos2, out):
             interleave(nc.scalar.copy, x0_staged[h][:, 0:PASS0_SCALAR], x_raw[0, h][:, :, 0:PASS0_SCALAR])
             interleave(nc.vector.tensor_copy, x0_staged[h][:, PASS0_SCALAR:HALF], x_raw[0, h][:, :, PASS0_SCALAR:HALF])
             quantize_tokens(0, h, x0_staged[h])
-        slot_words = [gather_words(0)]
+        gather_words(slot_words[0][:], 0, 0, SLOTS - C, WINDOW)
 
         x1_staged = [keep.tile([P, HALF, PACK], BF16, name=f"x1_staged{h}", align_bytes=64) for h in range(2)]
+        cut = HALF - PASS1_GPSIMD
+        interleave(nc.scalar.copy, x1_staged[0][:], x_raw[1, 0][:])
+        interleave(nc.scalar.copy, x1_staged[1][:, 0:cut], x_raw[1, 1][:, :, 0:cut])
+        nc.gpsimd.tensor_copy(out=x1_staged[1][:, cut:HALF], in_=x_raw[1, 1][:, :, cut:HALF].rearrange("p j c -> p c j"))
         for h in range(2):
-            interleave(nc.scalar.copy, x1_staged[h][:], x_raw[1, h][:])
             quantize_tokens(1, h, x1_staged[h])
-        slot_words.append(gather_words(1))
+        last_words = keep.tile([P, C], U32, name="last_words", tag="x_raw11", align_bytes=BURST)
+        gather_words(last_words[:], 0, SLOTS - C, SLOTS, T)
+        gather_words(slot_words[1][:], 1, 0, SLOTS, WINDOW)
         slot_scales = [gather_scales(0, "slot_scales0")]
 
         w_words = keep.tile([P, E * PASSES * N], U32, name="w_words", align_bytes=64)
@@ -124,11 +131,10 @@ def tile_routed_moe_kernel(tc, xT, w, b, gate, offs, pos1, pos2, out):
         def stage(s):
             g = [s in group for group in GROUPS].index(True)
             if g not in staged:
-                tag = "w_raw0" if g == 0 else f"staged{g}"
-                staged[g] = keep.tile([P, len(GROUPS[g]), N, PACK], BF16, name=f"staged{g}", tag=tag, align_bytes=BURST)
+                staged[g] = keep.tile([P, len(GROUPS[g]), N, PACK], BF16, name=f"staged{g}", align_bytes=BURST)
             dst = staged[g][:, GROUPS[g].index(s)]
             if s in GPSIMD_STEPS:
-                nc.gpsimd.tensor_scalar(dst, w_raw[s].rearrange("p j n -> p n j"), 1.0, 0.0, MULT, ADD)
+                nc.gpsimd.tensor_copy(out=dst, in_=w_raw[s].rearrange("p j n -> p n j"))
             elif s == last:
                 interleave(nc.scalar.copy, dst[:, 0:LAST_SCALAR], w_raw[s][:, :, 0:LAST_SCALAR])
             else:
@@ -164,7 +170,7 @@ def tile_routed_moe_kernel(tc, xT, w, b, gate, offs, pos1, pos2, out):
                 out=acc[e],
                 lhsT=w_words[:, cols].bitcast(FP8X4),
                 lhsT_scale=w_scales[:, cols],
-                rhs=slot_words[a][:, slots].bitcast(FP8X4),
+                rhs=(last_words[:] if s == last - 1 else slot_words[a][:, slots]).bitcast(FP8X4),
                 rhs_scale=slot_scales[h][PLANE_STEP * a : P, at * C : (at + 1) * C],
                 start=(a == 0),
                 stop=(a == PASSES - 1),

@@ -24,12 +24,14 @@ LIST_ROWS = 16
 PLANE_STEP = 4
 HALF = T // 2
 WINDOW = 1376
+BYTE_WINDOW = 896
+BYTE_EXPERTS = (range(0, 5), range(5, E))
 PASS0_SCALAR = 96
 LAST_SCALAR = 64
 W_LOADS = [(0, 2), (2, 3)] + [(s, 1) for s in range(5, E * PASSES)]
 GPSIMD_STEPS = (3, 4)
 PASS1_GPSIMD = 112
-GROUPS = [(2, 3, 4, 5), (0, 1, 6, 7), (8, 9, 10, 11), (12, 13), (14,), (15,)]
+GROUPS = [(2, 3, 4, 5), (0, 1, 6, 7), (8, 9), (10, 11), (12, 13), (14,), (15,)]
 BURST = 256
 JOINT = range(4, 7)
 
@@ -55,8 +57,8 @@ def tile_routed_moe_kernel(tc, xT, w, b, gate, offs, pos1, pos2, out):
         bias = keep.tile([P, E], F32, name="bias", align_bytes=BURST)
         gates = keep.tile([P, 2, T], F32, name="gates", align_bytes=BURST)
 
-        x_scales = keep.tile([P, WINDOW], U8, name="x_scales", align_bytes=64)
-        nc.gpsimd.memset(x_scales[:], 0)
+        x_scales = keep.tile([P, BYTE_WINDOW], U8, name="x_scales", align_bytes=64)
+        nc.gpsimd.memset(x_scales[:].bitcast(I32), 0)
         x_words = []
         for a in range(PASSES):
             words = keep.tile([P, WINDOW], I32, name=f"x_words{a}", align_bytes=64)
@@ -95,9 +97,10 @@ def tile_routed_moe_kernel(tc, xT, w, b, gate, offs, pos1, pos2, out):
             nc.vector.tensor_copy(out=dst, in_=x_words[a][:, 0:window].bitcast(U32).indirect(offsets))
 
         def gather_scales(h, tag):
-            gathered = keep.tile([P, SLOTS // 2], U8, name=f"slot_scales{h}", tag=tag, align_bytes=BURST)
-            columns = SLOTS // 2 // LIST_ROWS
-            nc.vector.tensor_copy(out=gathered[:], in_=x_scales[:].indirect(offs_t[:, h * columns : (h + 1) * columns]))
+            experts = BYTE_EXPERTS[h]
+            gathered = keep.tile([P, len(experts) * C], U8, name=f"slot_scales{h}", tag=tag, align_bytes=BURST)
+            offsets = offs_t[:, experts.start * C // LIST_ROWS : experts.stop * C // LIST_ROWS]
+            nc.vector.tensor_copy(out=gathered[:], in_=x_scales[:].indirect(offsets))
             return gathered
 
         x0_staged = [keep.tile([P, HALF, PACK], BF16, name=f"x0_staged{h}", align_bytes=64) for h in range(2)]
@@ -153,18 +156,20 @@ def tile_routed_moe_kernel(tc, xT, w, b, gate, offs, pos1, pos2, out):
             stage(s)
         quantize_weights(0, staged[0])
         quantize_weights(1, staged[1])
-        slot_scales.append(gather_scales(1, "w_raw7"))
         quantize_weights(2, staged[2])
+        slot_scales.append(gather_scales(1, "w_raw9"))
         quantize_weights(3, staged[3])
-        interleave(nc.vector.tensor_copy, staged[5][:, 0, LAST_SCALAR:N], w_raw[last][:, :, LAST_SCALAR:N])
-        y = keep.tile([P, SLOTS], F32, name="y", tag=f"w_raw{last}", align_bytes=BURST)
         quantize_weights(4, staged[4])
+        interleave(nc.vector.tensor_copy, staged[6][:, 0, LAST_SCALAR:N], w_raw[last][:, :, LAST_SCALAR:N])
+        y = keep.tile([P, SLOTS], F32, name="y", tag=f"w_raw{last}", align_bytes=BURST)
         quantize_weights(5, staged[5])
+        quantize_weights(6, staged[6])
 
         for s in sorted(place, key=place.get):
             e, a = divmod(s, PASSES)
             slots = slice(e * C, (e + 1) * C)
-            h, at = divmod(e, E // 2)
+            h = int(e in BYTE_EXPERTS[1])
+            at = e - BYTE_EXPERTS[h].start
             cols = slice(place[s] * N, (place[s] + 1) * N)
             nc.tensor.matmul_mx(
                 out=acc[e],

@@ -15,6 +15,7 @@ FP8X4 = mybir.dt.float8_e4m3fn_x4
 MULT = mybir.AluOpType.mult
 ADD = mybir.AluOpType.add
 IDENTITY = mybir.ActivationFunctionType.Identity
+COPY = mybir.ActivationFunctionType.Copy
 
 P = 128
 PACK = 4
@@ -195,9 +196,10 @@ def tile_routed_moe_kernel(tc, xT, w, b, gate, offs, pos1, pos2, out):
         halves = ((0, HALF), (HALF, T))
         second_parts = []
         for lo, hi in halves:
+            fetched = keep.tile([P, hi - lo], F32, name=f"fetched{lo}")
+            nc.scalar.activation(fetched[:], y[:].indirect(pos2_t[:, lo // LIST_ROWS : hi // LIST_ROWS]), COPY)
             part = keep.tile([P, hi - lo], F32, name=f"second_part{lo}")
-            offsets = pos2_t[:, lo // LIST_ROWS : hi // LIST_ROWS]
-            nc.vector.tensor_tensor(part[:], y[:].indirect(offsets), gates[:, 1, lo:hi], MULT)
+            nc.vector.tensor_mul(part[:], fetched[:], gates[:, 1, lo:hi])
             second_parts.append(part)
         for (lo, hi), part in zip(halves, second_parts):
             total = keep.tile([P, hi - lo], F32, name=f"total{lo}", align_bytes=BURST)

@@ -21,6 +21,8 @@ P = 128
 PACK = 4
 PASSES = K // (P * PACK)
 SLOTS = E * C
+STEPS = E * PASSES
+LAST_STEP = STEPS - 1
 LIST_ROWS = 16
 PLANE_STEP = 4
 HALF = T // 2
@@ -28,10 +30,10 @@ WINDOW = 1376
 BYTE_WINDOW = 896
 BYTE_EXPERTS = (range(0, 5), range(5, E))
 PASS0_SCALAR = 96
-LAST_SCALAR = 64
-W_LOADS = [(0, 2), (2, 3)] + [(s, 1) for s in range(5, E * PASSES)]
-GPSIMD_STEPS = (3, 4)
 PASS1_GPSIMD = 112
+LAST_SCALAR = 64
+W_LOADS = [(0, 2), (2, 3)] + [(s, 1) for s in range(5, STEPS)]
+GPSIMD_STEPS = (3, 4)
 GROUPS = [(2, 3, 4, 5), (0, 1, 6, 7), (8, 9), (10, 11), (12, 13), (14,), (15,)]
 BURST = 256
 JOINT = range(4, 7)
@@ -42,11 +44,20 @@ def tile_routed_moe_kernel(tc, xT, w, b, gate, offs, pos1, pos2, out):
     x_view = xT.rearrange("(a p j) t -> a p j t", p=P, j=PACK)
     w_view = w.rearrange("e (a p j) n -> p (e a) (j n)", p=P, j=PACK)
 
-    def interleave(copy, dst, src):
-        if len(src.shape) == 3:
-            copy(out=dst.rearrange("p (c i) j -> p c j i", i=4), in_=src.rearrange("p j (c i) -> p c j i", i=4))
-        else:
-            copy(out=dst.rearrange("p a (c i) j -> p a c j i", i=4), in_=src.rearrange("p a j (c i) -> p a c j i", i=4))
+    def interleave(copy, run, dst, src):
+        copy(out=dst.rearrange("p (c i) j -> p c j i", i=run), in_=src.rearrange("p j (c i) -> p c j i", i=run))
+
+    def interleave_scalar(dst, src):
+        interleave(nc.scalar.copy, 2, dst, src)
+
+    def interleave_vector(dst, src):
+        interleave(nc.vector.tensor_copy, 4, dst, src)
+
+    def interleave_gpsimd(dst, src):
+        nc.gpsimd.tensor_copy(out=dst, in_=src.rearrange("p j c -> p c j"))
+
+    def entries(list_tile, lo, hi):
+        return list_tile[:, lo // LIST_ROWS : hi // LIST_ROWS]
 
     with ExitStack() as ctx:
         keep = ctx.enter_context(tc.tile_pool(name="keep", bufs=1))
@@ -91,31 +102,32 @@ def tile_routed_moe_kernel(tc, xT, w, b, gate, offs, pos1, pos2, out):
                 in_=staged[:].rearrange("p t j -> p (t j)"),
             )
 
-        slot_words = [keep.tile([P, SLOTS - C * (1 - a)], U32, name=f"slot_words{a}", align_bytes=64) for a in range(PASSES)]
+        slot_words = [
+            keep.tile([P, SLOTS - C * (1 - a)], U32, name=f"slot_words{a}", align_bytes=64) for a in range(PASSES)
+        ]
 
         def gather_words(dst, a, lo, hi, window):
-            offsets = offs_t[:, lo // LIST_ROWS : hi // LIST_ROWS]
-            nc.vector.tensor_copy(out=dst, in_=x_words[a][:, 0:window].bitcast(U32).indirect(offsets))
+            nc.vector.tensor_copy(out=dst, in_=x_words[a][:, 0:window].bitcast(U32).indirect(entries(offs_t, lo, hi)))
 
-        def gather_scales(h, tag):
-            experts = BYTE_EXPERTS[h]
-            gathered = keep.tile([P, len(experts) * C], U8, name=f"slot_scales{h}", tag=tag, align_bytes=BURST)
-            offsets = offs_t[:, experts.start * C // LIST_ROWS : experts.stop * C // LIST_ROWS]
+        def gather_scales(part, tag):
+            experts = BYTE_EXPERTS[part]
+            gathered = keep.tile([P, len(experts) * C], U8, name=f"slot_scales{part}", tag=tag, align_bytes=BURST)
+            offsets = entries(offs_t, experts.start * C, experts.stop * C)
             nc.vector.tensor_copy(out=gathered[:], in_=x_scales[:].indirect(offsets))
             return gathered
 
         x0_staged = [keep.tile([P, HALF, PACK], BF16, name=f"x0_staged{h}", align_bytes=64) for h in range(2)]
         for h in range(2):
-            interleave(nc.scalar.copy, x0_staged[h][:, 0:PASS0_SCALAR], x_raw[0, h][:, :, 0:PASS0_SCALAR])
-            interleave(nc.vector.tensor_copy, x0_staged[h][:, PASS0_SCALAR:HALF], x_raw[0, h][:, :, PASS0_SCALAR:HALF])
+            interleave_scalar(x0_staged[h][:, 0:PASS0_SCALAR], x_raw[0, h][:, :, 0:PASS0_SCALAR])
+            interleave_vector(x0_staged[h][:, PASS0_SCALAR:HALF], x_raw[0, h][:, :, PASS0_SCALAR:HALF])
             quantize_tokens(0, h, x0_staged[h])
         gather_words(slot_words[0][:], 0, 0, SLOTS - C, WINDOW)
 
         x1_staged = [keep.tile([P, HALF, PACK], BF16, name=f"x1_staged{h}", align_bytes=64) for h in range(2)]
         cut = HALF - PASS1_GPSIMD
-        interleave(nc.scalar.copy, x1_staged[0][:], x_raw[1, 0][:])
-        interleave(nc.scalar.copy, x1_staged[1][:, 0:cut], x_raw[1, 1][:, :, 0:cut])
-        nc.gpsimd.tensor_copy(out=x1_staged[1][:, cut:HALF], in_=x_raw[1, 1][:, :, cut:HALF].rearrange("p j c -> p c j"))
+        interleave_scalar(x1_staged[0][:], x_raw[1, 0][:])
+        interleave_scalar(x1_staged[1][:, 0:cut], x_raw[1, 1][:, :, 0:cut])
+        interleave_gpsimd(x1_staged[1][:, cut:HALF], x_raw[1, 1][:, :, cut:HALF])
         for h in range(2):
             quantize_tokens(1, h, x1_staged[h])
         last_words = keep.tile([P, C], U32, name="last_words", tag="x_raw11", align_bytes=BURST)
@@ -123,61 +135,64 @@ def tile_routed_moe_kernel(tc, xT, w, b, gate, offs, pos1, pos2, out):
         gather_words(slot_words[1][:], 1, 0, SLOTS, WINDOW)
         slot_scales = [gather_scales(0, "slot_scales0")]
 
-        w_words = keep.tile([P, E * PASSES * N], U32, name="w_words", align_bytes=64)
-        w_scales = keep.tile([P, E * PASSES * N], U8, name="w_scales", align_bytes=64)
+        w_words = keep.tile([P, STEPS * N], U32, name="w_words", align_bytes=64)
+        w_scales = keep.tile([P, STEPS * N], U8, name="w_scales", align_bytes=64)
         place = {s: i for i, s in enumerate(s for group in GROUPS for s in group)}
         joint = psum.tile([P, len(JOINT), C], F32, name="joint")
-        acc = [joint[:, e - JOINT.start] if e in JOINT else psum.tile([P, C], F32, name=f"acc{e}")[:] for e in range(E)]
-        last = E * PASSES - 1
+        acc = [
+            joint[:, e - JOINT.start] if e in JOINT else psum.tile([P, C], F32, name=f"acc{e}")[:] for e in range(E)
+        ]
 
-        staged = {}
+        w_staged = {}
 
         def stage(s):
             g = [s in group for group in GROUPS].index(True)
-            if g not in staged:
-                staged[g] = keep.tile([P, len(GROUPS[g]), N, PACK], BF16, name=f"staged{g}", align_bytes=BURST)
-            dst = staged[g][:, GROUPS[g].index(s)]
+            if g not in w_staged:
+                w_staged[g] = keep.tile([P, len(GROUPS[g]), N, PACK], BF16, name=f"staged{g}", align_bytes=BURST)
+            dst = w_staged[g][:, GROUPS[g].index(s)]
             if s in GPSIMD_STEPS:
-                nc.gpsimd.tensor_copy(out=dst, in_=w_raw[s].rearrange("p j n -> p n j"))
-            elif s == last:
-                interleave(nc.scalar.copy, dst[:, 0:LAST_SCALAR], w_raw[s][:, :, 0:LAST_SCALAR])
+                interleave_gpsimd(dst, w_raw[s])
+            elif s == LAST_STEP:
+                interleave_scalar(dst[:, 0:LAST_SCALAR], w_raw[s][:, :, 0:LAST_SCALAR])
             else:
-                interleave(nc.scalar.copy, dst, w_raw[s])
+                interleave_scalar(dst, w_raw[s])
 
-        def quantize_weights(g, staged):
+        def quantize_weights(g):
             first = place[GROUPS[g][0]] * N
             cols = slice(first, first + len(GROUPS[g]) * N)
             nc.vector.quantize_mx(
                 out=w_words[:, cols].bitcast(FP8X4),
                 scales=w_scales[:, cols],
-                in_=staged[:].rearrange("p a n j -> p (a n j)"),
+                in_=w_staged[g][:].rearrange("p s n j -> p (s n j)"),
             )
 
-        for s in range(E * PASSES):
+        for s in range(STEPS):
             stage(s)
-        quantize_weights(0, staged[0])
-        quantize_weights(1, staged[1])
-        quantize_weights(2, staged[2])
-        slot_scales.append(gather_scales(1, "w_raw9"))
-        quantize_weights(3, staged[3])
-        quantize_weights(4, staged[4])
-        interleave(nc.vector.tensor_copy, staged[6][:, 0, LAST_SCALAR:N], w_raw[last][:, :, LAST_SCALAR:N])
-        y = keep.tile([P, SLOTS], F32, name="y", tag=f"w_raw{last}", align_bytes=BURST)
-        quantize_weights(5, staged[5])
-        quantize_weights(6, staged[6])
+        early_steps = BYTE_EXPERTS[0].stop * PASSES
+        early_groups = [g for g, group in enumerate(GROUPS) if max(group) < early_steps]
+        last_group = len(GROUPS) - 1
+        for g in early_groups:
+            quantize_weights(g)
+        slot_scales.append(gather_scales(1, f"w_raw{early_steps - 1}"))
+        for g in range(len(early_groups), last_group - 1):
+            quantize_weights(g)
+        interleave_vector(w_staged[last_group][:, 0, LAST_SCALAR:N], w_raw[LAST_STEP][:, :, LAST_SCALAR:N])
+        y = keep.tile([P, SLOTS], F32, name="y", tag=f"w_raw{LAST_STEP}", align_bytes=BURST)
+        quantize_weights(last_group - 1)
+        quantize_weights(last_group)
 
         for s in sorted(place, key=place.get):
             e, a = divmod(s, PASSES)
             slots = slice(e * C, (e + 1) * C)
-            h = int(e in BYTE_EXPERTS[1])
-            at = e - BYTE_EXPERTS[h].start
+            part = int(e in BYTE_EXPERTS[1])
+            at = e - BYTE_EXPERTS[part].start
             cols = slice(place[s] * N, (place[s] + 1) * N)
             nc.tensor.matmul_mx(
                 out=acc[e],
                 lhsT=w_words[:, cols].bitcast(FP8X4),
                 lhsT_scale=w_scales[:, cols],
-                rhs=(last_words[:] if s == last - 1 else slot_words[a][:, slots]).bitcast(FP8X4),
-                rhs_scale=slot_scales[h][PLANE_STEP * a : P, at * C : (at + 1) * C],
+                rhs=(last_words[:] if (e, a) == (E - 1, 0) else slot_words[a][:, slots]).bitcast(FP8X4),
+                rhs_scale=slot_scales[part][PLANE_STEP * a : P, at * C : (at + 1) * C],
                 start=(a == 0),
                 stop=(a == PASSES - 1),
             )
@@ -197,11 +212,11 @@ def tile_routed_moe_kernel(tc, xT, w, b, gate, offs, pos1, pos2, out):
         second_parts = []
         for lo, hi in halves:
             fetched = keep.tile([P, hi - lo], F32, name=f"fetched{lo}")
-            nc.scalar.activation(fetched[:], y[:].indirect(pos2_t[:, lo // LIST_ROWS : hi // LIST_ROWS]), COPY)
-            part = keep.tile([P, hi - lo], F32, name=f"second_part{lo}")
-            nc.vector.tensor_mul(part[:], fetched[:], gates[:, 1, lo:hi])
-            second_parts.append(part)
-        for (lo, hi), part in zip(halves, second_parts):
+            nc.scalar.activation(fetched[:], y[:].indirect(entries(pos2_t, lo, hi)), COPY)
+            product = keep.tile([P, hi - lo], F32, name=f"second_part{lo}")
+            nc.vector.tensor_mul(product[:], fetched[:], gates[:, 1, lo:hi])
+            second_parts.append(product)
+        for (lo, hi), product in zip(halves, second_parts):
             total = keep.tile([P, hi - lo], F32, name=f"total{lo}", align_bytes=BURST)
-            nc.vector.tensor_add(total[:], first_part[:, lo:hi], part[:])
+            nc.vector.tensor_add(total[:], first_part[:, lo:hi], product[:])
             nc.sync.dma_start(out=out[:, lo:hi], in_=total[:])

from contextlib import ExitStack

import concourse.mybir as mybir

K, T, E, C, N = 1024, 512, 8, 128, 128
FLOPS = 2 * K * E * C * N

F32 = mybir.dt.float32
BF16 = mybir.dt.bfloat16
U32 = mybir.dt.uint32
I32 = mybir.dt.int32
U16 = mybir.dt.uint16
U8 = mybir.dt.uint8
FP8X4 = mybir.dt.float8_e4m3fn_x4
MULT = mybir.AluOpType.mult
ADD = mybir.AluOpType.add
IDENTITY = mybir.ActivationFunctionType.Identity
COPY = mybir.ActivationFunctionType.Copy

P = 128
PACK = 4
PASSES = K // (P * PACK)
SLOTS = E * C
STEPS = E * PASSES
LAST_STEP = STEPS - 1
LIST_ROWS = 16
PLANE_STEP = 4
HALF = T // 2
WINDOW = 1376
BYTE_WINDOW = 896
BYTE_EXPERTS = (range(0, 5), range(5, E))
PASS0_SCALAR = 96
PASS1_GPSIMD = 112
LAST_SCALAR = 64
W_LOADS = [(0, 2), (2, 3)] + [(s, 1) for s in range(5, STEPS)]
GPSIMD_STEPS = (3, 4)
GROUPS = [(2, 3, 4, 5), (0, 1, 6, 7), (8, 9), (10, 11), (12, 13), (14,), (15,)]
BURST = 256
JOINT = range(4, 7)


def tile_routed_moe_kernel(tc, xT, w, b, gate, offs, pos1, pos2, out):
    nc = tc.nc
    x_view = xT.rearrange("(a p j) t -> a p j t", p=P, j=PACK)
    w_view = w.rearrange("e (a p j) n -> p (e a) (j n)", p=P, j=PACK)

    def interleave(copy, run, dst, src):
        copy(out=dst.rearrange("p (c i) j -> p c j i", i=run), in_=src.rearrange("p j (c i) -> p c j i", i=run))

    def interleave_scalar(dst, src):
        interleave(nc.scalar.copy, 2, dst, src)

    def interleave_vector(dst, src):
        interleave(nc.vector.tensor_copy, 4, dst, src)

    def interleave_gpsimd(dst, src):
        nc.gpsimd.tensor_copy(out=dst, in_=src.rearrange("p j c -> p c j"))

    def entries(list_tile, lo, hi):
        return list_tile[:, lo // LIST_ROWS : hi // LIST_ROWS]

    with ExitStack() as ctx:
        keep = ctx.enter_context(tc.tile_pool(name="keep", bufs=1))
        psum = ctx.enter_context(tc.psum_pool(name="psum", bufs=1))

        offs_t = keep.tile([P, SLOTS // LIST_ROWS], U16, name="offs_t", align_bytes=BURST)
        pos1_t = keep.tile([P, T // LIST_ROWS], U16, name="pos1_t", align_bytes=BURST)
        pos2_t = keep.tile([P, T // LIST_ROWS], U16, name="pos2_t", align_bytes=BURST)
        bias = keep.tile([P, E], F32, name="bias", align_bytes=BURST)
        gates = keep.tile([P, 2, T], F32, name="gates", align_bytes=BURST)

        x_scales = keep.tile([P, BYTE_WINDOW], U8, name="x_scales", align_bytes=64)
        nc.gpsimd.memset(x_scales[:].bitcast(I32), 0)
        x_words = []
        for a in range(PASSES):
            words = keep.tile([P, WINDOW], I32, name=f"x_words{a}", align_bytes=64)
            nc.vector.memset(words[:, T:WINDOW], 0)
            x_words.append(words)

        x_raw = {}
        for a in range(PASSES):
            for h in range(2):
                x_raw[a, h] = keep.tile([P, PACK, HALF], F32, name=f"x_raw{a}{h}", tag=f"x_raw{a}{h}", align_bytes=BURST)
                nc.sync.dma_start(out=x_raw[a, h][:], in_=x_view[a][:, :, h * HALF : (h + 1) * HALF])
            if a == 0:
                nc.sync.dma_start(offs_t[:], offs)
        w_raw = []
        for first, count in W_LOADS:
            raw = keep.tile([P, count, PACK, N], F32, name=f"w_raw{first}", tag=f"w_raw{first}", align_bytes=BURST)
            nc.sync.dma_start(out=raw[:].rearrange("p s j n -> p s (j n)"), in_=w_view[:, first : first + count])
            w_raw.extend(raw[:, s] for s in range(count))
        nc.sync.dma_start(bias[:], b)
        nc.sync.dma_start(pos1_t[:], pos1)
        nc.sync.dma_start(gates[:], gate.rearrange("r p t -> p r t"))
        nc.sync.dma_start(pos2_t[:], pos2)

        def quantize_tokens(a, h, staged):
            cols = slice(h * HALF, (h + 1) * HALF)
            nc.vector.quantize_mx(
                out=x_words[a][:, cols].bitcast(FP8X4),
                scales=x_scales[PLANE_STEP * a : P, cols],
                in_=staged[:].rearrange("p t j -> p (t j)"),
            )

        slot_words = [
            keep.tile([P, SLOTS - C * (1 - a)], U32, name=f"slot_words{a}", align_bytes=64) for a in range(PASSES)
        ]

        def gather_words(dst, a, lo, hi, window):
            nc.vector.tensor_copy(out=dst, in_=x_words[a][:, 0:window].bitcast(U32).indirect(entries(offs_t, lo, hi)))

        def gather_scales(part, tag):
            experts = BYTE_EXPERTS[part]
            gathered = keep.tile([P, len(experts) * C], U8, name=f"slot_scales{part}", tag=tag, align_bytes=BURST)
            offsets = entries(offs_t, experts.start * C, experts.stop * C)
            nc.vector.tensor_copy(out=gathered[:], in_=x_scales[:].indirect(offsets))
            return gathered

        x0_staged = [keep.tile([P, HALF, PACK], BF16, name=f"x0_staged{h}", align_bytes=64) for h in range(2)]
        for h in range(2):
            interleave_scalar(x0_staged[h][:, 0:PASS0_SCALAR], x_raw[0, h][:, :, 0:PASS0_SCALAR])
            interleave_vector(x0_staged[h][:, PASS0_SCALAR:HALF], x_raw[0, h][:, :, PASS0_SCALAR:HALF])
            quantize_tokens(0, h, x0_staged[h])
        gather_words(slot_words[0][:], 0, 0, SLOTS - C, WINDOW)

        x1_staged = [keep.tile([P, HALF, PACK], BF16, name=f"x1_staged{h}", align_bytes=64) for h in range(2)]
        cut = HALF - PASS1_GPSIMD
        interleave_scalar(x1_staged[0][:], x_raw[1, 0][:])
        interleave_scalar(x1_staged[1][:, 0:cut], x_raw[1, 1][:, :, 0:cut])
        interleave_gpsimd(x1_staged[1][:, cut:HALF], x_raw[1, 1][:, :, cut:HALF])
        for h in range(2):
            quantize_tokens(1, h, x1_staged[h])
        last_words = keep.tile([P, C], U32, name="last_words", tag="x_raw11", align_bytes=BURST)
        gather_words(last_words[:], 0, SLOTS - C, SLOTS, T)
        gather_words(slot_words[1][:], 1, 0, SLOTS, WINDOW)
        slot_scales = [gather_scales(0, "slot_scales0")]

        w_words = keep.tile([P, STEPS * N], U32, name="w_words", align_bytes=64)
        w_scales = keep.tile([P, STEPS * N], U8, name="w_scales", align_bytes=64)
        place = {s: i for i, s in enumerate(s for group in GROUPS for s in group)}
        joint = psum.tile([P, len(JOINT), C], F32, name="joint")
        acc = [
            joint[:, e - JOINT.start] if e in JOINT else psum.tile([P, C], F32, name=f"acc{e}")[:] for e in range(E)
        ]

        w_staged = {}

        def stage(s):
            g = [s in group for group in GROUPS].index(True)
            if g not in w_staged:
                w_staged[g] = keep.tile([P, len(GROUPS[g]), N, PACK], BF16, name=f"staged{g}", align_bytes=BURST)
            dst = w_staged[g][:, GROUPS[g].index(s)]
            if s in GPSIMD_STEPS:
                interleave_gpsimd(dst, w_raw[s])
            elif s == LAST_STEP:
                interleave_scalar(dst[:, 0:LAST_SCALAR], w_raw[s][:, :, 0:LAST_SCALAR])
            else:
                interleave_scalar(dst, w_raw[s])

        def quantize_weights(g):
            first = place[GROUPS[g][0]] * N
            cols = slice(first, first + len(GROUPS[g]) * N)
            nc.vector.quantize_mx(
                out=w_words[:, cols].bitcast(FP8X4),
                scales=w_scales[:, cols],
                in_=w_staged[g][:].rearrange("p s n j -> p (s n j)"),
            )

        for s in range(STEPS):
            stage(s)
        early_steps = BYTE_EXPERTS[0].stop * PASSES
        early_groups = [g for g, group in enumerate(GROUPS) if max(group) < early_steps]
        last_group = len(GROUPS) - 1
        for g in early_groups:
            quantize_weights(g)
        slot_scales.append(gather_scales(1, f"w_raw{early_steps - 1}"))
        for g in range(len(early_groups), last_group - 1):
            quantize_weights(g)
        interleave_vector(w_staged[last_group][:, 0, LAST_SCALAR:N], w_raw[LAST_STEP][:, :, LAST_SCALAR:N])
        y = keep.tile([P, SLOTS], F32, name="y", tag=f"w_raw{LAST_STEP}", align_bytes=BURST)
        quantize_weights(last_group - 1)
        quantize_weights(last_group)

        for s in sorted(place, key=place.get):
            e, a = divmod(s, PASSES)
            slots = slice(e * C, (e + 1) * C)
            part = int(e in BYTE_EXPERTS[1])
            at = e - BYTE_EXPERTS[part].start
            cols = slice(place[s] * N, (place[s] + 1) * N)
            nc.tensor.matmul_mx(
                out=acc[e],
                lhsT=w_words[:, cols].bitcast(FP8X4),
                lhsT_scale=w_scales[:, cols],
                rhs=(last_words[:] if (e, a) == (E - 1, 0) else slot_words[a][:, slots]).bitcast(FP8X4),
                rhs_scale=slot_scales[part][PLANE_STEP * a : P, at * C : (at + 1) * C],
                start=(a == 0),
                stop=(a == PASSES - 1),
            )
        for e in range(E):
            if e not in JOINT:
                nc.scalar.activation(y[:, e * C : (e + 1) * C], acc[e], IDENTITY, bias=bias[:, e : e + 1])
        nc.vector.tensor_tensor(
            y[:, JOINT.start * C : JOINT.stop * C].rearrange("p (e c) -> p e c", c=C),
            joint[:],
            bias[:, JOINT.start : JOINT.stop].unsqueeze(2).to_broadcast([P, len(JOINT), C]),
            ADD,
        )

        first_part = keep.tile([P, T], F32, name="first_part")
        nc.vector.tensor_tensor(first_part[:], y[:].indirect(pos1_t[:]), gates[:, 0], MULT)
        halves = ((0, HALF), (HALF, T))
        second_parts = []
        for lo, hi in halves:
            fetched = keep.tile([P, hi - lo], F32, name=f"fetched{lo}")
            nc.scalar.activation(fetched[:], y[:].indirect(entries(pos2_t, lo, hi)), COPY)
            product = keep.tile([P, hi - lo], F32, name=f"second_part{lo}")
            nc.vector.tensor_mul(product[:], fetched[:], gates[:, 1, lo:hi])
            second_parts.append(product)
        for (lo, hi), product in zip(halves, second_parts):
            total = keep.tile([P, hi - lo], F32, name=f"total{lo}", align_bytes=BURST)
            nc.vector.tensor_add(total[:], first_part[:, lo:hi], product[:])
            nc.sync.dma_start(out=out[:, lo:hi], in_=total[:])
